import numpy as np
import ml_dtypes


def mxq(x, axis, fmt="e4m3"):
    dtype, down = {"e4m3": (ml_dtypes.float8_e4m3fn, 7), "e5m2": (ml_dtypes.float8_e5m2, 14)}[fmt]
    v = np.moveaxis(np.asarray(x, np.float32).astype(ml_dtypes.bfloat16).astype(np.float64), axis, -1)
    blocks = v.reshape(v.shape[:-1] + (-1, 32))
    amax = np.abs(blocks).max(-1, keepdims=True)
    byte = np.maximum(np.where(amax > 0, np.frexp(amax)[1] - 1 + 127, 0) - down, 1)
    scale = np.exp2(byte - 127.0)
    codes = (blocks / scale).astype(np.float32).astype(dtype).astype(np.float64)
    return np.moveaxis((codes * scale).reshape(v.shape), -1, axis)


WIDE = False


def mx_kscale(k):
    if not WIDE:
        return np.ones(k)
    levels = np.array([10, -10, 5, -5, 0])
    if k % 512:
        return np.exp2(np.random.permutation(np.resize(levels, k // 32))).repeat(32)
    a = np.empty((k // 512, 16))
    for p in range(k // 512):
        a[p, :8] = np.random.permutation(np.resize(levels, 8))
        for g in range(8):
            far = levels[np.abs(levels - a[p, g]) >= 10]
            a[p, g + 8] = far[np.random.randint(len(far))]
    return np.exp2(a.ravel()).repeat(32)


BF16 = ml_dtypes.bfloat16


def bf(x):
    return np.asarray(x, np.float32).astype(BF16)


def f64(x):
    return np.asarray(x).astype(np.float64)


E2M1 = np.array([0.0, 0.5, 1.0, 1.5, 2.0, 3.0, 4.0, 6.0, -0.0, -0.5, -1.0, -1.5, -2.0, -3.0, -4.0, -6.0])


def pack_weight(w, fmt):
    k, n = w.shape
    w = f64(bf(w)).reshape(k // 32, 32, n)
    amax = np.abs(w).max(1)
    if fmt == "e4m3":
        byte = np.frexp(amax)[1] - 1 + 127 - 7
    else:
        mant, ex = np.frexp(amax / 6.0)
        byte = np.where(mant > 0.5, ex, ex - 1) + 127
    byte = np.clip(np.where(amax > 0, byte, 1), 1, 254)
    scaled = (w * np.exp2(127.0 - byte)[:, None, :]).reshape(k, n).astype(np.float32)
    by_word = np.ascontiguousarray(scaled.reshape(k // 512, 128, 4, n).transpose(0, 1, 3, 2))
    if fmt == "e4m3":
        words = by_word.astype(ml_dtypes.float8_e4m3fn).view(np.uint8)
    else:
        c = by_word.astype(ml_dtypes.float4_e2m1fn).view(np.uint8) & 0xF
        words = c[..., 0::2] | (c[..., 1::2] << 4)
    return np.ascontiguousarray(words), np.ascontiguousarray(byte.astype(np.uint8).reshape(k // 512, 16, n))


def unpack_weight(words, scales, fmt):
    g, p, n, _ = words.shape
    if fmt == "e4m3":
        vals = np.ascontiguousarray(words).view(ml_dtypes.float8_e4m3fn).astype(np.float64)
    else:
        nib = np.empty((g, p, n, 4), np.uint8)
        nib[..., 0::2] = words & 0xF
        nib[..., 1::2] = words >> 4
        vals = E2M1[nib]
    vals = vals * np.repeat(np.exp2(scales.astype(np.float64) - 127.0), 8, axis=1)[..., None]
    return vals.transpose(0, 1, 3, 2).reshape(g * 512, n)
def pack4(w):
    words, scales = pack_weight(w, "e2m1")
    return words.reshape(words.shape[0], 128, -1), scales


def unpack4(words, scales):
    return unpack_weight(words.reshape(words.shape[0], 128, -1, 2), scales, "e2m1")


M, K, N = 768, 1024, 2048


def setup_inputs():
    s = mx_kscale(K)
    w_base = 1.5 * np.random.standard_normal((K, N)) / np.sqrt(K) / s[:, None]
    w_domain = 2.0 * np.random.standard_normal((K, N)) / np.sqrt(K) / s[:, None]
    w_gate = 2.0 * np.random.standard_normal((K, N)) / np.sqrt(K) / s[:, None]
    base_words, base_scales = pack4(w_base)
    domain_words, domain_scales = pack_weight(w_domain, "e4m3")
    return {"z": bf(np.random.standard_normal((M, K))),
            "scale": bf((1 + 0.1 * np.random.standard_normal(K)) * s),
            "base_words": base_words, "base_scales": base_scales,
            "domain_words": domain_words, "domain_scales": domain_scales,
            "w_gate": bf(w_gate),
            "resid": bf(np.random.standard_normal((M, N)))}


def reference(z, scale, base_words, base_scales, domain_words, domain_scales, w_gate, resid):
    zf = f64(z)
    act = 0.5 * zf * (1.0 + np.tanh(np.sqrt(2.0 / np.pi) * (zf + 0.044715 * zf ** 3)))
    a = mxq(act * f64(scale), 1, "e4m3")
    base = a @ unpack4(base_words, base_scales)
    domain = a @ unpack_weight(domain_words, domain_scales, "e4m3")
    gate = a @ mxq(f64(w_gate), 0, "e4m3")
    return f64(resid) + base + domain * (1.0 / (1.0 + np.exp(-gate)))

@@ -1,0 +1,435 @@
+from contextlib import ExitStack
+import concourse.mybir as mybir
+from concourse.masks import make_identity
+
+M, K, N = 768, 1024, 2048
+FLOPS = 3 * 2 * M * K * N
+F32 = mybir.dt.float32
+BF16 = mybir.dt.bfloat16
+U32 = mybir.dt.uint32
+I32 = mybir.dt.int32
+U8 = mybir.dt.uint8
+E4M3X4 = mybir.dt.float8_e4m3fn_x4
+E2M1X4 = mybir.dt.float4_e2m1fn_x4
+ACT = mybir.ActivationFunctionType
+ALU = mybir.AluOpType
+P = 128
+PLAN = [
+    ("load_z", 0,),
+    ("init",),
+    ("load_scales", "d", 0, "Y",),
+    ("load_scales", "d", 1, "Y",),
+    ("load_scales", "d", 2, "Y",),
+    ("load_scales", "d", 3, "Y",),
+    ("load_scales", "b", 0, "G",),
+    ("load_scales", "b", 1, "G",),
+    ("load_scales", "b", 2, "G",),
+    ("load_scales", "b", 3, "G",),
+    ("load_z", 1,),
+    ("load_w", 0, 0,),
+    ("load_w", 0, 1,),
+    ("load_b", 0,),
+    ("load_d", 0,),
+    ("load_z", 2,),
+    ("load_z", 3,),
+    ("load_z", 4,),
+    ("load_z", 5,),
+    ("load_r", 0,),
+    ("load_w", 1, 0,),
+    ("load_w", 1, 1,),
+    ("load_d", 1,),
+    ("load_b", 1,),
+    ("load_r", 1,),
+    ("load_w", 2, 0,),
+    ("load_w", 2, 1,),
+    ("load_d", 2,),
+    ("load_b", 2,),
+    ("load_r", 2,),
+    ("load_w", 3, 0,),
+    ("load_w", 3, 1,),
+    ("load_d", 3,),
+    ("load_b", 3,),
+    ("load_r", 3,),
+    ("gelu", 0,),
+    ("turn", 0,),
+    ("lay", 0, 0, "V",),
+    ("gelu", 1,),
+    ("turn", 1,),
+    ("lay", 0, 1, "V",),
+    ("lay", 0, 3, "S",),
+    ("weigh", 0,),
+    ("quant_w", 0, 0,),
+    ("lay", 0, 2, "S",),
+    ("quant_a", 0,),
+    ("quant_w", 0, 1,),
+    ("quant_w", 0, 3,),
+    ("weigh", 1,),
+    ("quant_w", 0, 2,),
+    ("product", "d", 0, 0,),
+    ("gelu", 2,),
+    ("quant_a", 1,),
+    ("product", "b", 0, 0,),
+    ("turn", 2,),
+    ("product", "g", 0, 0,),
+    ("gelu", 3,),
+    ("squash", 0, 0,),
+    ("weigh", 2,),
+    ("quant_a", 2,),
+    ("gated", 0, 0,),
+    ("turn", 3,),
+    ("product", "g", 1, 0,),
+    ("product", "d", 1, 0,),
+    ("product", "b", 1, 0,),
+    ("lay", 1, 2, "G",),
+    ("gelu", 4,),
+    ("squash", 1, 0,),
+    ("weigh", 3,),
+    ("summed", 0, 0,),
+    ("finish", 0, 0, "G",),
+    ("store", 0, 0,),
+    ("quant_a", 3,),
+    ("gated", 1, 0,),
+    ("turn", 4,),
+    ("product", "g", 2, 0,),
+    ("product", "d", 2, 0,),
+    ("product", "b", 2, 0,),
+    ("lay", 1, 1, "S",),
+    ("gelu", 5,),
+    ("squash", 2, 0,),
+    ("weigh", 4,),
+    ("summed", 1, 0,),
+    ("finish", 1, 0, "G",),
+    ("store", 1, 0,),
+    ("quant_w", 1, 2,),
+    ("quant_a", 4,),
+    ("gated", 2, 0,),
+    ("turn", 5,),
+    ("product", "g", 3, 0,),
+    ("product", "d", 3, 0,),
+    ("product", "b", 3, 0,),
+    ("lay", 1, 0, "S",),
+    ("lay", 1, 3, "S",),
+    ("squash", 3, 0,),
+    ("weigh", 5,),
+    ("summed", 2, 0,),
+    ("finish", 2, 0, "G",),
+    ("store", 2, 0,),
+    ("quant_w", 1, 1,),
+    ("quant_a", 5,),
+    ("gated", 3, 0,),
+    ("product", "g", 4, 0,),
+    ("product", "d", 4, 0,),
+    ("product", "b", 4, 0,),
+    ("squash", 4, 0,),
+    ("summed", 3, 0,),
+    ("finish", 3, 0, "G",),
+    ("store", 3, 0,),
+    ("quant_w", 1, 0,),
+    ("quant_w", 1, 3,),
+    ("gated", 4, 0,),
+    ("product", "g", 5, 0,),
+    ("product", "d", 5, 0,),
+    ("product", "b", 5, 0,),
+    ("squash", 5, 0,),
+    ("summed", 4, 0,),
+    ("finish", 4, 0, "G",),
+    ("store", 4, 0,),
+    ("gated", 5, 0,),
+    ("product", "g", 0, 1,),
+    ("product", "d", 0, 1,),
+    ("product", "b", 0, 1,),
+    ("squash", 0, 1,),
+    ("summed", 5, 0,),
+    ("finish", 5, 0, "G",),
+    ("store", 5, 0,),
+    ("gated", 0, 1,),
+    ("product", "g", 1, 1,),
+    ("product", "d", 1, 1,),
+    ("product", "b", 1, 1,),
+    ("lay", 2, 2, "G",),
+    ("squash", 1, 1,),
+    ("summed", 0, 1,),
+    ("finish", 0, 1, "G",),
+    ("store", 0, 1,),
+    ("gated", 1, 1,),
+    ("product", "g", 2, 1,),
+    ("product", "d", 2, 1,),
+    ("product", "b", 2, 1,),
+    ("lay", 2, 1, "S",),
+    ("squash", 2, 1,),
+    ("summed", 1, 1,),
+    ("finish", 1, 1, "G",),
+    ("store", 1, 1,),
+    ("quant_w", 2, 2,),
+    ("gated", 2, 1,),
+    ("product", "g", 3, 1,),
+    ("product", "d", 3, 1,),
+    ("product", "b", 3, 1,),
+    ("lay", 2, 0, "S",),
+    ("lay", 2, 3, "S",),
+    ("squash", 3, 1,),
+    ("summed", 2, 1,),
+    ("finish", 2, 1, "G",),
+    ("store", 2, 1,),
+    ("quant_w", 2, 1,),
+    ("gated", 3, 1,),
+    ("product", "g", 4, 1,),
+    ("product", "d", 4, 1,),
+    ("product", "b", 4, 1,),
+    ("squash", 4, 1,),
+    ("summed", 3, 1,),
+    ("finish", 3, 1, "G",),
+    ("store", 3, 1,),
+    ("quant_w", 2, 0,),
+    ("quant_w", 2, 3,),
+    ("gated", 4, 1,),
+    ("product", "g", 5, 1,),
+    ("product", "d", 5, 1,),
+    ("product", "b", 5, 1,),
+    ("squash", 5, 1,),
+    ("summed", 4, 1,),
+    ("finish", 4, 1, "G",),
+    ("store", 4, 1,),
+    ("gated", 5, 1,),
+    ("product", "g", 0, 2,),
+    ("product", "d", 0, 2,),
+    ("product", "b", 0, 2,),
+    ("squash", 0, 2,),
+    ("summed", 5, 1,),
+    ("finish", 5, 1, "G",),
+    ("store", 5, 1,),
+    ("gated", 0, 2,),
+    ("product", "g", 1, 2,),
+    ("product", "d", 1, 2,),
+    ("product", "b", 1, 2,),
+    ("lay", 3, 2, "G",),
+    ("squash", 1, 2,),
+    ("summed", 0, 2,),
+    ("finish", 0, 2, "G",),
+    ("store", 0, 2,),
+    ("gated", 1, 2,),
+    ("product", "g", 2, 2,),
+    ("product", "d", 2, 2,),
+    ("product", "b", 2, 2,),
+    ("lay", 3, 1, "S",),
+    ("squash", 2, 2,),
+    ("summed", 1, 2,),
+    ("finish", 1, 2, "G",),
+    ("store", 1, 2,),
+    ("quant_w", 3, 2,),
+    ("gated", 2, 2,),
+    ("product", "g", 3, 2,),
+    ("product", "d", 3, 2,),
+    ("product", "b", 3, 2,),
+    ("lay", 3, 0, "S",),
+    ("lay", 3, 3, "S",),
+    ("squash", 3, 2,),
+    ("summed", 2, 2,),
+    ("finish", 2, 2, "G",),
+    ("store", 2, 2,),
+    ("quant_w", 3, 1,),
+    ("gated", 3, 2,),
+    ("product", "g", 4, 2,),
+    ("product", "d", 4, 2,),
+    ("product", "b", 4, 2,),
+    ("squash", 4, 2,),
+    ("summed", 3, 2,),
+    ("finish", 3, 2, "G",),
+    ("store", 3, 2,),
+    ("quant_w", 3, 0,),
+    ("quant_w", 3, 3,),
+    ("gated", 4, 2,),
+    ("product", "g", 5, 2,),
+    ("product", "d", 5, 2,),
+    ("product", "b", 5, 2,),
+    ("squash", 5, 2,),
+    ("summed", 4, 2,),
+    ("finish", 4, 2, "G",),
+    ("store", 4, 2,),
+    ("gated", 5, 2,),
+    ("product", "g", 0, 3,),
+    ("product", "d", 0, 3,),
+    ("product", "b", 0, 3,),
+    ("squash", 0, 3,),
+    ("summed", 5, 2,),
+    ("finish", 5, 2, "G",),
+    ("store", 5, 2,),
+    ("gated", 0, 3,),
+    ("product", "g", 1, 3,),
+    ("product", "d", 1, 3,),
+    ("product", "b", 1, 3,),
+    ("squash", 1, 3,),
+    ("summed", 0, 3,),
+    ("finish", 0, 3, "G",),
+    ("store", 0, 3,),
+    ("gated", 1, 3,),
+    ("product", "g", 2, 3,),
+    ("product", "d", 2, 3,),
+    ("product", "b", 2, 3,),
+    ("squash", 2, 3,),
+    ("summed", 1, 3,),
+    ("finish", 1, 3, "G",),
+    ("store", 1, 3,),
+    ("gated", 2, 3,),
+    ("product", "g", 3, 3,),
+    ("product", "d", 3, 3,),
+    ("product", "b", 3, 3,),
+    ("squash", 3, 3,),
+    ("summed", 2, 3,),
+    ("finish", 2, 3, "G",),
+    ("store", 2, 3,),
+    ("gated", 3, 3,),
+    ("product", "g", 4, 3,),
+    ("product", "d", 4, 3,),
+    ("product", "b", 4, 3,),
+    ("squash", 4, 3,),
+    ("summed", 3, 3,),
+    ("finish", 3, 3, "G",),
+    ("store", 3, 3,),
+    ("gated", 4, 3,),
+    ("product", "g", 5, 3,),
+    ("product", "d", 5, 3,),
+    ("product", "b", 5, 3,),
+    ("squash", 5, 3,),
+    ("summed", 4, 3,),
+    ("finish", 4, 3, "G",),
+    ("store", 4, 3,),
+    ("gated", 5, 3,),
+    ("summed", 5, 3,),
+    ("finish", 5, 3, "V",),
+    ("store", 5, 3,),
+]
+GROUPS = 2
+PACK = 4
+TILES = 6
+CHUNKS = 4
+WIDTH = 512
+PIECE = 256
+
+
+def tile_gated_adapter_up_s10_kernel(tc, z, scale, base_words, base_scales, domain_words, domain_scales, w_gate, resid, out):
+    nc = tc.nc
+    with ExitStack() as ctx:
+        keep = ctx.enter_context(tc.tile_pool(name="keep", bufs=1))
+        work = ctx.enter_context(tc.tile_pool(name="work", bufs=4))
+        psum = ctx.enter_context(tc.psum_pool(name="psum", bufs=8))
+        ctx.enter_context(tc.manual_schedule())
+
+        ident = keep.tile([P, P], F32, name="ident")
+        warm = keep.tile([P, 1], F32, name="warm")
+        scale_col = keep.tile([P, GROUPS, PACK], BF16, name="scale_col")
+        z_raw = [keep.tile([P, K], BF16, name=f"z{m}") for m in range(TILES)]
+        a_codes = [keep.tile([P, GROUPS * P], U32, name=f"ac{m}", align_bytes=64) for m in range(TILES)]
+        a_scales = [keep.tile([P, GROUPS * P], U8, name=f"as{m}", align_bytes=64) for m in range(TILES)]
+        w_raw = [[keep.tile([P, PACK, WIDTH], BF16, name=f"w{c}{g}") for g in range(GROUPS)] for c in range(CHUNKS)]
+        w_codes = [keep.tile([P, GROUPS, WIDTH], U32, name=f"wc{c}", align_bytes=64) for c in range(CHUNKS)]
+        w_scales = [keep.tile([P, GROUPS, WIDTH], U8, name=f"ws{c}", align_bytes=64) for c in range(CHUNKS)]
+        b_codes = [keep.tile([P, GROUPS, 2 * WIDTH], U8, name=f"bc{c}", align_bytes=64) for c in range(CHUNKS)]
+        d_codes = [keep.tile([P, GROUPS, 4 * WIDTH], U8, name=f"dc{c}", align_bytes=64) for c in range(CHUNKS)]
+        b_planes = keep.tile([P, GROUPS, N], U8, name="b_planes", align_bytes=64)
+        d_planes = keep.tile([P, GROUPS, N], U8, name="d_planes", align_bytes=64)
+        r_raw = [keep.tile([P, TILES, WIDTH], BF16, name=f"r{c}") for c in range(CHUNKS)]
+
+        gel, a_bf, banks, w_il, tanh, fold, done = {}, {}, {}, {}, {}, {}, {}
+
+        def load_z(m):
+            nc.sync.dma_start(out=z_raw[m][:], in_=z[m * P:(m + 1) * P, :])
+
+        def load_w(c, g):
+            nc.sync.dma_start(out=w_raw[c][g][:], in_=w_gate[512 * g:512 * (g + 1), c * WIDTH:(c + 1) * WIDTH].rearrange("(p j) n -> p j n", j=PACK))
+
+        def load_b(c):
+            nc.sync.dma_start(out=b_codes[c][:], in_=base_words[:, :, 2 * WIDTH * c:2 * WIDTH * (c + 1)].rearrange("g p b -> p g b"))
+
+        def load_d(c):
+            nc.sync.dma_start(out=d_codes[c][:], in_=domain_words[:, :, WIDTH * c:WIDTH * (c + 1), :].rearrange("g p n t -> p g (n t)"))
+
+        def load_r(c):
+            nc.sync.dma_start(out=r_raw[c][:], in_=resid[:, WIDTH * c:WIDTH * (c + 1)].rearrange("(m p) n -> p m n", p=P))
+
+        def load_scales(kind, q, eng):
+            planes, src = (d_planes, domain_scales) if kind == "d" else (b_planes, base_scales)
+            queue = {"G": nc.gpsimd, "S": nc.scalar, "Y": nc.sync}[eng]
+            queue.dma_start(out=planes[32 * q:32 * q + 4].bitcast(I32), in_=src.bitcast(I32)[:, 4 * q:4 * q + 4, :].rearrange("g r n -> r g n"))
+
+        def init():
+            nc.scalar.dma_start(out=scale_col[:], in_=scale.rearrange("(g p t) -> p g t", p=P, t=PACK))
+            nc.vector.memset(warm[:], 0.0)
+            nc.scalar.activation(out=warm[:], in_=warm[:], func=ACT.Gelu_apprx_tanh)
+            nc.vector.memset(d_planes[:].rearrange("p g n -> p (g n)").bitcast(I32), 0)
+            nc.vector.memset(b_planes[:].rearrange("p g n -> p (g n)").bitcast(I32), 0)
+            make_identity(nc, ident[:])
+
+        def gelu(m):
+            gel[m] = work.tile([P, GROUPS, PACK, P], F32, tag="gel", name="gel", bufs=2)
+            nc.scalar.activation(out=gel[m][:], in_=z_raw[m][:].rearrange("r (g p t) -> r g t p", g=GROUPS, t=PACK), func=ACT.Gelu_apprx_tanh)
+
+        def turn(m):
+            for g in range(GROUPS):
+                banks["a", m, g] = psum.tile([P, PACK, P], F32, tag="bank", name="bank")
+                for t in range(PACK):
+                    nc.tensor.transpose(banks["a", m, g][:, t, :], gel[m][:, g, t, :], ident[:])
+
+        def weigh(m):
+            a_bf[m] = work.tile([P, GROUPS, P, PACK], BF16, tag="a_bf", name="a_bf", bufs=2, align_bytes=64)
+            for g in range(GROUPS):
+                nc.vector.tensor_tensor(out=a_bf[m][:, g], in0=banks["a", m, g][:].rearrange("p t r -> p r t"), in1=scale_col[:, g, :].unsqueeze(1).to_broadcast([P, P, PACK]), op=ALU.mult)
+
+        def quant_a(m):
+            nc.vector.quantize_mx(out=a_codes[m][:].bitcast(E4M3X4), scales=a_scales[m][:], in_=a_bf[m][:].rearrange("p g r t -> p (g r t)"))
+
+        def lay(c, k, eng):
+            g, h = divmod(k, 2)
+            il = work.tile([P, PIECE, PACK], BF16, tag="w_il", name="w_il", align_bytes=64)
+            w_il[c, k] = il
+            src = w_raw[c][g][:, :, PIECE * h:PIECE * (h + 1)].rearrange("p j n -> p n j")
+            if eng == "S":
+                nc.scalar.copy(out=il[:], in_=src)
+            elif eng == "V":
+                nc.vector.tensor_copy(out=il[:], in_=src)
+            else:
+                nc.gpsimd.tensor_scalar(out=il[:], in0=src, scalar1=1.0, scalar2=0.0, op0=ALU.mult, op1=ALU.add)
+
+        def quant_w(c, k):
+            g, h = divmod(k, 2)
+            cols = slice(PIECE * h, PIECE * (h + 1))
+            nc.vector.quantize_mx(out=w_codes[c][:, g, cols].bitcast(E4M3X4), scales=w_scales[c][:, g, cols], in_=w_il[c, k][:].rearrange("p n j -> p (n j)"))
+
+        def product(kind, m, c):
+            bank = psum.tile([P, WIDTH], F32, tag="bank", name="bank")
+            banks[kind, m, c] = bank
+            for g in range(GROUPS):
+                if kind == "g":
+                    rhs, rs = w_codes[c][:, g, :].bitcast(E4M3X4), w_scales[c][:, g, :]
+                elif kind == "d":
+                    rhs, rs = d_codes[c][:, g, :].bitcast(E4M3X4), d_planes[:, g, WIDTH * c:WIDTH * (c + 1)]
+                else:
+                    rhs, rs = b_codes[c][:, g, :].bitcast(E2M1X4), b_planes[:, g, WIDTH * c:WIDTH * (c + 1)]
+                nc.tensor.matmul_mx(out=bank[:], lhsT=a_codes[m][:, g * P:(g + 1) * P].bitcast(E4M3X4), lhsT_scale=a_scales[m][:, g * P:(g + 1) * P], rhs=rhs, rhs_scale=rs, start=(g == 0), stop=(g == GROUPS - 1))
+
+        def squash(m, c):
+            t = work.tile([P, WIDTH], F32, tag="tanh", name="tanh", bufs=3)
+            tanh[m, c] = t
+            nc.scalar.activation(out=t[:], in_=banks["g", m, c][:], func=ACT.Tanh, scale=0.5)
+
+        def gated(m, c):
+            v = work.tile([P, WIDTH], F32, tag="fold", name="fold", bufs=3)
+            fold[m, c] = v
+            nc.vector.scalar_tensor_tensor(out=v[:], in0=tanh[m, c][:], scalar=1.0, in1=banks["d", m, c][:], op0=ALU.add, op1=ALU.mult)
+
+        def summed(m, c):
+            y = work.tile([P, WIDTH], F32, tag="done", name="done", bufs=12)
+            done[m, c] = y
+            nc.vector.scalar_tensor_tensor(out=y[:], in0=fold[m, c][:], scalar=0.5, in1=banks["b", m, c][:], op0=ALU.mult, op1=ALU.add)
+
+        def finish(m, c, eng):
+            y = done[m, c]
+            e = nc.gpsimd if eng == "G" else nc.vector
+            e.tensor_tensor(out=y[:], in0=y[:], in1=r_raw[c][:, m, :], op=ALU.add)
+
+        def store(m, c):
+            nc.sync.dma_start(out=out[m * P:(m + 1) * P, c * WIDTH:(c + 1) * WIDTH], in_=done[m, c][:])
+
+        ops = dict(init=init, load_scales=load_scales, load_z=load_z, load_w=load_w, load_b=load_b, load_d=load_d, load_r=load_r, gelu=gelu, turn=turn, weigh=weigh, quant_a=quant_a, lay=lay, quant_w=quant_w, product=product, squash=squash, gated=gated, summed=summed, finish=finish, store=store)
+        for step in PLAN:
+            ops[step[0]](*step[1:])

@@ -15,106 +15,106 @@ ACT = mybir.ActivationFunctionType
 ALU = mybir.AluOpType
 P = 128
 PLAN = [
-    ("load_z", 0,),
     ("init",),
-    ("load_scales", "d", 0, "Y",),
-    ("load_scales", "d", 1, "Y",),
-    ("load_scales", "d", 2, "Y",),
-    ("load_scales", "d", 3, "Y",),
-    ("load_scales", "b", 0, "G",),
-    ("load_scales", "b", 1, "G",),
-    ("load_scales", "b", 2, "G",),
-    ("load_scales", "b", 3, "G",),
-    ("load_z", 1,),
+    ("load_z", 0,),
     ("load_w", 0, 0,),
+    ("lay", 0, 0, "V",),
+    ("load_scales", "d", 0, "S",),
+    ("load_scales", "d", 1, "S",),
+    ("load_z", 1,),
     ("load_w", 0, 1,),
-    ("load_b", 0,),
+    ("load_scales", "d", 2, "S",),
+    ("load_scales", "d", 3, "S",),
     ("load_d", 0,),
+    ("load_scales", "b", 0, "Y",),
     ("load_z", 2,),
+    ("turn", 0,),
+    ("turn", 1,),
+    ("load_scales", "b", 1, "Y",),
+    ("load_b", 0,),
+    ("load_scales", "b", 2, "Y",),
     ("load_z", 3,),
+    ("load_scales", "b", 3, "Y",),
     ("load_z", 4,),
     ("load_z", 5,),
     ("load_r", 0,),
+    ("gelu", 0,),
+    ("weigh", 0, "V",),
+    ("gelu", 1,),
+    ("lay", 0, 2, "S",),
+    ("quant_w", 0, 0,),
     ("load_w", 1, 0,),
     ("load_w", 1, 1,),
+    ("lay", 0, 3, "S",),
     ("load_d", 1,),
     ("load_b", 1,),
     ("load_r", 1,),
     ("load_w", 2, 0,),
     ("load_w", 2, 1,),
     ("load_d", 2,),
+    ("turn", 2,),
     ("load_b", 2,),
     ("load_r", 2,),
     ("load_w", 3, 0,),
+    ("lay", 0, 1, "V",),
     ("load_w", 3, 1,),
     ("load_d", 3,),
     ("load_b", 3,),
-    ("load_r", 3,),
-    ("gelu", 0,),
-    ("turn", 0,),
-    ("lay", 0, 0, "V",),
-    ("gelu", 1,),
-    ("turn", 1,),
-    ("lay", 0, 1, "V",),
-    ("lay", 0, 3, "S",),
-    ("weigh", 0,),
-    ("quant_w", 0, 0,),
-    ("lay", 0, 2, "S",),
+    ("weigh", 1, "V",),
     ("quant_a", 0,),
-    ("quant_w", 0, 1,),
-    ("quant_w", 0, 3,),
-    ("weigh", 1,),
-    ("quant_w", 0, 2,),
-    ("product", "d", 0, 0,),
     ("gelu", 2,),
+    ("product", "d", 0, 0,),
+    ("quant_w", 0, 1,),
+    ("load_r", 3,),
+    ("quant_w", 0, 2,),
+    ("quant_w", 0, 3,),
     ("quant_a", 1,),
-    ("product", "b", 0, 0,),
-    ("turn", 2,),
+    ("turn", 3,),
     ("product", "g", 0, 0,),
+    ("product", "b", 0, 0,),
     ("gelu", 3,),
     ("squash", 0, 0,),
-    ("weigh", 2,),
+    ("weigh", 2, "V",),
     ("quant_a", 2,),
     ("gated", 0, 0,),
-    ("turn", 3,),
+    ("turn", 4,),
     ("product", "g", 1, 0,),
     ("product", "d", 1, 0,),
     ("product", "b", 1, 0,),
-    ("lay", 1, 2, "G",),
     ("gelu", 4,),
     ("squash", 1, 0,),
-    ("weigh", 3,),
+    ("lay", 1, 1, "S",),
+    ("lay", 1, 2, "S",),
+    ("weigh", 3, "G",),
     ("summed", 0, 0,),
     ("finish", 0, 0, "G",),
     ("store", 0, 0,),
     ("quant_a", 3,),
     ("gated", 1, 0,),
-    ("turn", 4,),
+    ("turn", 5,),
     ("product", "g", 2, 0,),
     ("product", "d", 2, 0,),
     ("product", "b", 2, 0,),
-    ("lay", 1, 1, "S",),
     ("gelu", 5,),
     ("squash", 2, 0,),
-    ("weigh", 4,),
+    ("weigh", 4, "V",),
     ("summed", 1, 0,),
     ("finish", 1, 0, "G",),
     ("store", 1, 0,),
+    ("quant_w", 1, 1,),
     ("quant_w", 1, 2,),
     ("quant_a", 4,),
     ("gated", 2, 0,),
-    ("turn", 5,),
     ("product", "g", 3, 0,),
     ("product", "d", 3, 0,),
     ("product", "b", 3, 0,),
+    ("squash", 3, 0,),
     ("lay", 1, 0, "S",),
     ("lay", 1, 3, "S",),
-    ("squash", 3, 0,),
-    ("weigh", 5,),
+    ("weigh", 5, "V",),
     ("summed", 2, 0,),
     ("finish", 2, 0, "G",),
     ("store", 2, 0,),
-    ("quant_w", 1, 1,),
     ("quant_a", 5,),
     ("gated", 3, 0,),
     ("product", "g", 4, 0,),
@@ -146,8 +146,9 @@ PLAN = [
     ("product", "g", 1, 1,),
     ("product", "d", 1, 1,),
     ("product", "b", 1, 1,),
-    ("lay", 2, 2, "G",),
     ("squash", 1, 1,),
+    ("lay", 2, 1, "S",),
+    ("lay", 2, 2, "S",),
     ("summed", 0, 1,),
     ("finish", 0, 1, "G",),
     ("store", 0, 1,),
@@ -155,23 +156,22 @@ PLAN = [
     ("product", "g", 2, 1,),
     ("product", "d", 2, 1,),
     ("product", "b", 2, 1,),
-    ("lay", 2, 1, "S",),
     ("squash", 2, 1,),
     ("summed", 1, 1,),
     ("finish", 1, 1, "G",),
     ("store", 1, 1,),
+    ("quant_w", 2, 1,),
     ("quant_w", 2, 2,),
     ("gated", 2, 1,),
     ("product", "g", 3, 1,),
     ("product", "d", 3, 1,),
     ("product", "b", 3, 1,),
+    ("squash", 3, 1,),
     ("lay", 2, 0, "S",),
     ("lay", 2, 3, "S",),
-    ("squash", 3, 1,),
     ("summed", 2, 1,),
     ("finish", 2, 1, "G",),
     ("store", 2, 1,),
-    ("quant_w", 2, 1,),
     ("gated", 3, 1,),
     ("product", "g", 4, 1,),
     ("product", "d", 4, 1,),
@@ -202,8 +202,9 @@ PLAN = [
     ("product", "g", 1, 2,),
     ("product", "d", 1, 2,),
     ("product", "b", 1, 2,),
-    ("lay", 3, 2, "G",),
     ("squash", 1, 2,),
+    ("lay", 3, 1, "S",),
+    ("lay", 3, 2, "S",),
     ("summed", 0, 2,),
     ("finish", 0, 2, "G",),
     ("store", 0, 2,),
@@ -211,23 +212,22 @@ PLAN = [
     ("product", "g", 2, 2,),
     ("product", "d", 2, 2,),
     ("product", "b", 2, 2,),
-    ("lay", 3, 1, "S",),
     ("squash", 2, 2,),
     ("summed", 1, 2,),
     ("finish", 1, 2, "G",),
     ("store", 1, 2,),
+    ("quant_w", 3, 1,),
     ("quant_w", 3, 2,),
     ("gated", 2, 2,),
     ("product", "g", 3, 2,),
     ("product", "d", 3, 2,),
     ("product", "b", 3, 2,),
+    ("squash", 3, 2,),
     ("lay", 3, 0, "S",),
     ("lay", 3, 3, "S",),
-    ("squash", 3, 2,),
     ("summed", 2, 2,),
     ("finish", 2, 2, "G",),
     ("store", 2, 2,),
-    ("quant_w", 3, 1,),
     ("gated", 3, 2,),
     ("product", "g", 4, 2,),
     ("product", "d", 4, 2,),
@@ -360,20 +360,28 @@ def tile_gated_adapter_up_s10_kernel(tc, z, scale, base_words, base_scales, doma
             nc.vector.memset(b_planes[:].rearrange("p g n -> p (g n)").bitcast(I32), 0)
             make_identity(nc, ident[:])
 
-        def gelu(m):
-            gel[m] = work.tile([P, GROUPS, PACK, P], F32, tag="gel", name="gel", bufs=2)
-            nc.scalar.activation(out=gel[m][:], in_=z_raw[m][:].rearrange("r (g p t) -> r g t p", g=GROUPS, t=PACK), func=ACT.Gelu_apprx_tanh)
-
         def turn(m):
+            bank = psum.tile([P, GROUPS, 2, P], F32, tag="bank", name="bank")
+            banks["a", m] = bank
+            words = z_raw[m][:].bitcast(F32)
             for g in range(GROUPS):
-                banks["a", m, g] = psum.tile([P, PACK, P], F32, tag="bank", name="bank")
-                for t in range(PACK):
-                    nc.tensor.transpose(banks["a", m, g][:, t, :], gel[m][:, g, t, :], ident[:])
+                for u in range(2):
+                    nc.tensor.transpose(bank[:, g, u, :], words[:, 256 * g + u:256 * (g + 1):2], ident[:])
 
-        def weigh(m):
-            a_bf[m] = work.tile([P, GROUPS, P, PACK], BF16, tag="a_bf", name="a_bf", bufs=2, align_bytes=64)
+        def gelu(m):
+            gel[m] = work.tile([P, GROUPS, P, PACK], F32, tag="gel", name="gel", bufs=3)
+            pairs = banks["a", m][:].rearrange("p g u r -> p (g u r)").bitcast(BF16)
             for g in range(GROUPS):
-                nc.vector.tensor_tensor(out=a_bf[m][:, g], in0=banks["a", m, g][:].rearrange("p t r -> p r t"), in1=scale_col[:, g, :].unsqueeze(1).to_broadcast([P, P, PACK]), op=ALU.mult)
+                nc.scalar.activation(
+                    out=gel[m][:, g].rearrange("p r (u e) -> p r u e", u=2),
+                    in_=pairs[:, 512 * g:512 * (g + 1)].rearrange("p (u r e) -> p r u e", u=2, e=2),
+                    func=ACT.Gelu_apprx_tanh)
+
+        def weigh(m, eng="V"):
+            a_bf[m] = work.tile([P, GROUPS, P, PACK], BF16, tag="a_bf", name="a_bf", bufs=3, align_bytes=64)
+            e = nc.gpsimd if eng == "G" else nc.vector
+            for g in range(GROUPS):
+                e.tensor_tensor(out=a_bf[m][:, g], in0=gel[m][:, g], in1=scale_col[:, g, :].unsqueeze(1).to_broadcast([P, P, PACK]), op=ALU.mult)
 
         def quant_a(m):
             nc.vector.quantize_mx(out=a_codes[m][:].bitcast(E4M3X4), scales=a_scales[m][:], in_=a_bf[m][:].rearrange("p g r t -> p (g r t)"))
@@ -382,13 +390,14 @@ def tile_gated_adapter_up_s10_kernel(tc, z, scale, base_words, base_scales, doma
             g, h = divmod(k, 2)
             il = work.tile([P, PIECE, PACK], BF16, tag="w_il", name="w_il", align_bytes=64)
             w_il[c, k] = il
-            src = w_raw[c][g][:, :, PIECE * h:PIECE * (h + 1)].rearrange("p j n -> p n j")
+            src = w_raw[c][g][:, :, PIECE * h:PIECE * (h + 1)].rearrange("p j (q i) -> p q j i", i=4)
+            dst = il[:].rearrange("p (q i) j -> p q j i", i=4)
             if eng == "S":
-                nc.scalar.copy(out=il[:], in_=src)
+                nc.scalar.copy(out=dst, in_=src)
             elif eng == "V":
-                nc.vector.tensor_copy(out=il[:], in_=src)
+                nc.vector.tensor_copy(out=dst, in_=src)
             else:
-                nc.gpsimd.tensor_scalar(out=il[:], in0=src, scalar1=1.0, scalar2=0.0, op0=ALU.mult, op1=ALU.add)
+                nc.gpsimd.tensor_scalar(out=dst, in0=src, scalar1=1.0, scalar2=0.0, op0=ALU.mult, op1=ALU.add)
 
         def quant_w(c, k):
             g, h = divmod(k, 2)

@@ -17,8 +17,8 @@ P = 128
 PLAN = [
     ("init",),
     ("load_z", 0,),
+    ("turn", 0,),
     ("load_w", 0, 0,),
-    ("lay", 0, 0, "V",),
     ("load_scales", "d", 0, "S",),
     ("load_scales", "d", 1, "S",),
     ("load_z", 1,),
@@ -26,275 +26,269 @@ PLAN = [
     ("load_scales", "d", 2, "S",),
     ("load_scales", "d", 3, "S",),
     ("load_d", 0,),
-    ("load_scales", "b", 0, "Y",),
-    ("load_z", 2,),
-    ("turn", 0,),
     ("turn", 1,),
+    ("load_scales", "b", 0, "Y",),
+    ("gelu", 0,),
+    ("load_z", 2,),
     ("load_scales", "b", 1, "Y",),
     ("load_b", 0,),
+    ("lay", 0, 1, "V",),
     ("load_scales", "b", 2, "Y",),
-    ("load_z", 3,),
-    ("load_scales", "b", 3, "Y",),
-    ("load_z", 4,),
-    ("load_z", 5,),
-    ("load_r", 0,),
-    ("gelu", 0,),
     ("weigh", 0, "V",),
     ("gelu", 1,),
-    ("lay", 0, 2, "S",),
-    ("quant_w", 0, 0,),
+    ("load_z", 3,),
+    ("load_scales", "b", 3, "Y",),
+    ("lay", 0, 3, "S",),
+    ("quant_a", 0,),
     ("load_w", 1, 0,),
     ("load_w", 1, 1,),
-    ("lay", 0, 3, "S",),
+    ("load_r", 0,),
     ("load_d", 1,),
     ("load_b", 1,),
+    ("load_z", 4,),
+    ("load_z", 5,),
     ("load_r", 1,),
     ("load_w", 2, 0,),
     ("load_w", 2, 1,),
     ("load_d", 2,),
-    ("turn", 2,),
+    ("weigh", 1, "V",),
     ("load_b", 2,),
     ("load_r", 2,),
+    ("product", "d", 0, 0,),
+    ("quant_w", 0, 0, 1,),
+    ("lay", 0, 2, "S",),
+    ("lay", 0, 0, "V",),
     ("load_w", 3, 0,),
-    ("lay", 0, 1, "V",),
     ("load_w", 3, 1,),
     ("load_d", 3,),
     ("load_b", 3,),
-    ("weigh", 1, "V",),
-    ("quant_a", 0,),
-    ("gelu", 2,),
-    ("product", "d", 0, 0,),
-    ("quant_w", 0, 1,),
+    ("quant_w", 0, 1, 1,),
     ("load_r", 3,),
-    ("quant_w", 0, 2,),
-    ("quant_w", 0, 3,),
+    ("quant_w", 0, 1, 0,),
     ("quant_a", 1,),
+    ("quant_w", 0, 0, 0,),
+    ("turn", 2,),
     ("turn", 3,),
     ("product", "g", 0, 0,),
-    ("product", "b", 0, 0,),
-    ("gelu", 3,),
-    ("squash", 0, 0,),
-    ("weigh", 2, "V",),
-    ("quant_a", 2,),
-    ("gated", 0, 0,),
-    ("turn", 4,),
     ("product", "g", 1, 0,),
     ("product", "d", 1, 0,),
+    ("product", "b", 0, 0,),
     ("product", "b", 1, 0,),
-    ("gelu", 4,),
+    ("gelu", 2,),
+    ("gelu", 3,),
+    ("lay", 1, 2, "G",),
+    ("lay", 1, 0, "S",),
+    ("squash", 0, 0,),
     ("squash", 1, 0,),
-    ("lay", 1, 1, "S",),
-    ("lay", 1, 2, "S",),
-    ("weigh", 3, "G",),
+    ("weigh", 2, "V",),
+    ("weigh", 3, "V",),
+    ("quant_a", 2,),
+    ("quant_a", 3,),
+    ("gated", 0, 0,),
+    ("gated", 1, 0,),
     ("summed", 0, 0,),
     ("finish", 0, 0, "G",),
     ("store", 0, 0,),
-    ("quant_a", 3,),
-    ("gated", 1, 0,),
-    ("turn", 5,),
-    ("product", "g", 2, 0,),
-    ("product", "d", 2, 0,),
-    ("product", "b", 2, 0,),
-    ("gelu", 5,),
-    ("squash", 2, 0,),
-    ("weigh", 4, "V",),
     ("summed", 1, 0,),
     ("finish", 1, 0, "G",),
     ("store", 1, 0,),
-    ("quant_w", 1, 1,),
-    ("quant_w", 1, 2,),
-    ("quant_a", 4,),
-    ("gated", 2, 0,),
+    ("product", "g", 2, 0,),
     ("product", "g", 3, 0,),
+    ("product", "d", 2, 0,),
     ("product", "d", 3, 0,),
+    ("product", "b", 2, 0,),
     ("product", "b", 3, 0,),
-    ("squash", 3, 0,),
-    ("lay", 1, 0, "S",),
     ("lay", 1, 3, "S",),
-    ("weigh", 5, "V",),
+    ("lay", 1, 1, "S",),
+    ("squash", 2, 0,),
+    ("squash", 3, 0,),
+    ("quant_w", 1, 0,),
+    ("quant_w", 1, 1,),
+    ("gated", 2, 0,),
+    ("gated", 3, 0,),
     ("summed", 2, 0,),
     ("finish", 2, 0, "G",),
     ("store", 2, 0,),
-    ("quant_a", 5,),
-    ("gated", 3, 0,),
-    ("product", "g", 4, 0,),
-    ("product", "d", 4, 0,),
-    ("product", "b", 4, 0,),
-    ("squash", 4, 0,),
     ("summed", 3, 0,),
     ("finish", 3, 0, "G",),
     ("store", 3, 0,),
-    ("quant_w", 1, 0,),
-    ("quant_w", 1, 3,),
-    ("gated", 4, 0,),
-    ("product", "g", 5, 0,),
-    ("product", "d", 5, 0,),
-    ("product", "b", 5, 0,),
-    ("squash", 5, 0,),
-    ("summed", 4, 0,),
-    ("finish", 4, 0, "G",),
-    ("store", 4, 0,),
-    ("gated", 5, 0,),
+    ("turn", 4,),
+    ("turn", 5,),
     ("product", "g", 0, 1,),
-    ("product", "d", 0, 1,),
-    ("product", "b", 0, 1,),
-    ("squash", 0, 1,),
-    ("summed", 5, 0,),
-    ("finish", 5, 0, "G",),
-    ("store", 5, 0,),
-    ("gated", 0, 1,),
     ("product", "g", 1, 1,),
+    ("product", "d", 0, 1,),
     ("product", "d", 1, 1,),
+    ("product", "b", 0, 1,),
     ("product", "b", 1, 1,),
+    ("gelu", 4,),
+    ("gelu", 5,),
+    ("squash", 0, 1,),
     ("squash", 1, 1,),
-    ("lay", 2, 1, "S",),
-    ("lay", 2, 2, "S",),
+    ("weigh", 4, "V",),
+    ("weigh", 5, "V",),
+    ("quant_a", 4,),
+    ("quant_a", 5,),
+    ("gated", 0, 1,),
+    ("gated", 1, 1,),
     ("summed", 0, 1,),
     ("finish", 0, 1, "G",),
     ("store", 0, 1,),
-    ("gated", 1, 1,),
-    ("product", "g", 2, 1,),
-    ("product", "d", 2, 1,),
-    ("product", "b", 2, 1,),
-    ("squash", 2, 1,),
     ("summed", 1, 1,),
     ("finish", 1, 1, "G",),
     ("store", 1, 1,),
-    ("quant_w", 2, 1,),
-    ("quant_w", 2, 2,),
-    ("gated", 2, 1,),
+    ("product", "g", 2, 1,),
     ("product", "g", 3, 1,),
+    ("product", "d", 2, 1,),
     ("product", "d", 3, 1,),
+    ("product", "b", 2, 1,),
     ("product", "b", 3, 1,),
+    ("lay", 2, 2, "S",),
+    ("squash", 2, 1,),
     ("squash", 3, 1,),
-    ("lay", 2, 0, "S",),
-    ("lay", 2, 3, "S",),
+    ("gated", 2, 1,),
+    ("gated", 3, 1,),
     ("summed", 2, 1,),
     ("finish", 2, 1, "G",),
     ("store", 2, 1,),
-    ("gated", 3, 1,),
-    ("product", "g", 4, 1,),
-    ("product", "d", 4, 1,),
-    ("product", "b", 4, 1,),
-    ("squash", 4, 1,),
     ("summed", 3, 1,),
     ("finish", 3, 1, "G",),
     ("store", 3, 1,),
-    ("quant_w", 2, 0,),
-    ("quant_w", 2, 3,),
-    ("gated", 4, 1,),
+    ("product", "g", 4, 0,),
+    ("product", "g", 5, 0,),
+    ("product", "d", 4, 0,),
+    ("product", "d", 5, 0,),
+    ("product", "b", 4, 0,),
+    ("product", "b", 5, 0,),
+    ("lay", 2, 0, "S",),
+    ("squash", 4, 0,),
+    ("squash", 5, 0,),
+    ("gated", 4, 0,),
+    ("gated", 5, 0,),
+    ("summed", 4, 0,),
+    ("finish", 4, 0, "G",),
+    ("store", 4, 0,),
+    ("summed", 5, 0,),
+    ("finish", 5, 0, "G",),
+    ("store", 5, 0,),
+    ("product", "g", 4, 1,),
     ("product", "g", 5, 1,),
+    ("product", "d", 4, 1,),
     ("product", "d", 5, 1,),
+    ("product", "b", 4, 1,),
     ("product", "b", 5, 1,),
+    ("lay", 2, 3, "S",),
+    ("lay", 2, 1, "S",),
+    ("squash", 4, 1,),
     ("squash", 5, 1,),
+    ("quant_w", 2, 0,),
+    ("quant_w", 2, 1,),
+    ("gated", 4, 1,),
+    ("gated", 5, 1,),
     ("summed", 4, 1,),
     ("finish", 4, 1, "G",),
     ("store", 4, 1,),
-    ("gated", 5, 1,),
-    ("product", "g", 0, 2,),
-    ("product", "d", 0, 2,),
-    ("product", "b", 0, 2,),
-    ("squash", 0, 2,),
     ("summed", 5, 1,),
     ("finish", 5, 1, "G",),
     ("store", 5, 1,),
-    ("gated", 0, 2,),
+    ("product", "g", 0, 2,),
     ("product", "g", 1, 2,),
+    ("product", "d", 0, 2,),
     ("product", "d", 1, 2,),
+    ("product", "b", 0, 2,),
     ("product", "b", 1, 2,),
-    ("squash", 1, 2,),
-    ("lay", 3, 1, "S",),
     ("lay", 3, 2, "S",),
+    ("squash", 0, 2,),
+    ("squash", 1, 2,),
+    ("gated", 0, 2,),
+    ("gated", 1, 2,),
     ("summed", 0, 2,),
     ("finish", 0, 2, "G",),
     ("store", 0, 2,),
-    ("gated", 1, 2,),
-    ("product", "g", 2, 2,),
-    ("product", "d", 2, 2,),
-    ("product", "b", 2, 2,),
-    ("squash", 2, 2,),
     ("summed", 1, 2,),
     ("finish", 1, 2, "G",),
     ("store", 1, 2,),
-    ("quant_w", 3, 1,),
-    ("quant_w", 3, 2,),
-    ("gated", 2, 2,),
+    ("product", "g", 2, 2,),
     ("product", "g", 3, 2,),
+    ("product", "d", 2, 2,),
     ("product", "d", 3, 2,),
+    ("product", "b", 2, 2,),
     ("product", "b", 3, 2,),
-    ("squash", 3, 2,),
     ("lay", 3, 0, "S",),
-    ("lay", 3, 3, "S",),
+    ("squash", 2, 2,),
+    ("squash", 3, 2,),
+    ("gated", 2, 2,),
+    ("gated", 3, 2,),
     ("summed", 2, 2,),
     ("finish", 2, 2, "G",),
     ("store", 2, 2,),
-    ("gated", 3, 2,),
-    ("product", "g", 4, 2,),
-    ("product", "d", 4, 2,),
-    ("product", "b", 4, 2,),
-    ("squash", 4, 2,),
     ("summed", 3, 2,),
     ("finish", 3, 2, "G",),
     ("store", 3, 2,),
-    ("quant_w", 3, 0,),
-    ("quant_w", 3, 3,),
-    ("gated", 4, 2,),
+    ("product", "g", 4, 2,),
     ("product", "g", 5, 2,),
+    ("product", "d", 4, 2,),
     ("product", "d", 5, 2,),
+    ("product", "b", 4, 2,),
     ("product", "b", 5, 2,),
+    ("lay", 3, 3, "S",),
+    ("lay", 3, 1, "S",),
+    ("squash", 4, 2,),
     ("squash", 5, 2,),
+    ("quant_w", 3, 0,),
+    ("quant_w", 3, 1,),
+    ("gated", 4, 2,),
+    ("gated", 5, 2,),
     ("summed", 4, 2,),
     ("finish", 4, 2, "G",),
     ("store", 4, 2,),
-    ("gated", 5, 2,),
-    ("product", "g", 0, 3,),
-    ("product", "d", 0, 3,),
-    ("product", "b", 0, 3,),
-    ("squash", 0, 3,),
     ("summed", 5, 2,),
     ("finish", 5, 2, "G",),
     ("store", 5, 2,),
-    ("gated", 0, 3,),
+    ("product", "g", 0, 3,),
     ("product", "g", 1, 3,),
+    ("product", "d", 0, 3,),
     ("product", "d", 1, 3,),
+    ("product", "b", 0, 3,),
     ("product", "b", 1, 3,),
+    ("squash", 0, 3,),
     ("squash", 1, 3,),
+    ("gated", 0, 3,),
+    ("gated", 1, 3,),
     ("summed", 0, 3,),
     ("finish", 0, 3, "G",),
     ("store", 0, 3,),
-    ("gated", 1, 3,),
-    ("product", "g", 2, 3,),
-    ("product", "d", 2, 3,),
-    ("product", "b", 2, 3,),
-    ("squash", 2, 3,),
     ("summed", 1, 3,),
     ("finish", 1, 3, "G",),
     ("store", 1, 3,),
-    ("gated", 2, 3,),
+    ("product", "g", 2, 3,),
     ("product", "g", 3, 3,),
+    ("product", "d", 2, 3,),
     ("product", "d", 3, 3,),
+    ("product", "b", 2, 3,),
     ("product", "b", 3, 3,),
+    ("squash", 2, 3,),
     ("squash", 3, 3,),
+    ("gated", 2, 3,),
+    ("gated", 3, 3,),
     ("summed", 2, 3,),
     ("finish", 2, 3, "G",),
     ("store", 2, 3,),
-    ("gated", 3, 3,),
-    ("product", "g", 4, 3,),
-    ("product", "d", 4, 3,),
-    ("product", "b", 4, 3,),
-    ("squash", 4, 3,),
     ("summed", 3, 3,),
     ("finish", 3, 3, "G",),
     ("store", 3, 3,),
-    ("gated", 4, 3,),
+    ("product", "g", 4, 3,),
     ("product", "g", 5, 3,),
+    ("product", "d", 4, 3,),
     ("product", "d", 5, 3,),
+    ("product", "b", 4, 3,),
     ("product", "b", 5, 3,),
+    ("squash", 4, 3,),
     ("squash", 5, 3,),
+    ("gated", 4, 3,),
+    ("gated", 5, 3,),
     ("summed", 4, 3,),
     ("finish", 4, 3, "G",),
     ("store", 4, 3,),
-    ("gated", 5, 3,),
     ("summed", 5, 3,),
     ("finish", 5, 3, "V",),
     ("store", 5, 3,),
@@ -369,7 +363,7 @@ def tile_gated_adapter_up_s10_kernel(tc, z, scale, base_words, base_scales, doma
                     nc.tensor.transpose(bank[:, g, u, :], words[:, 256 * g + u:256 * (g + 1):2], ident[:])
 
         def gelu(m):
-            gel[m] = work.tile([P, GROUPS, P, PACK], F32, tag="gel", name="gel", bufs=3)
+            gel[m] = work.tile([P, GROUPS, P, PACK], F32, tag="gel", name="gel", bufs=6)
             pairs = banks["a", m][:].rearrange("p g u r -> p (g u r)").bitcast(BF16)
             for g in range(GROUPS):
                 nc.scalar.activation(
@@ -378,20 +372,24 @@ def tile_gated_adapter_up_s10_kernel(tc, z, scale, base_words, base_scales, doma
                     func=ACT.Gelu_apprx_tanh)
 
         def weigh(m, eng="V"):
-            a_bf[m] = work.tile([P, GROUPS, P, PACK], BF16, tag="a_bf", name="a_bf", bufs=3, align_bytes=64)
+            a_bf[m] = work.tile([P, GROUPS, P, PACK], BF16, tag="a_bf", name="a_bf", bufs=6, align_bytes=64)
             e = nc.gpsimd if eng == "G" else nc.vector
-            for g in range(GROUPS):
-                e.tensor_tensor(out=a_bf[m][:, g], in0=gel[m][:, g], in1=scale_col[:, g, :].unsqueeze(1).to_broadcast([P, P, PACK]), op=ALU.mult)
+            if eng == "G":
+                for g in range(GROUPS):
+                    e.tensor_tensor(out=a_bf[m][:, g], in0=gel[m][:, g], in1=scale_col[:, g, :].unsqueeze(1).to_broadcast([P, P, PACK]), op=ALU.mult)
+            else:
+                e.tensor_tensor(out=a_bf[m][:], in0=gel[m][:], in1=scale_col[:].unsqueeze(2).to_broadcast([P, GROUPS, P, PACK]), op=ALU.mult)
 
         def quant_a(m):
             nc.vector.quantize_mx(out=a_codes[m][:].bitcast(E4M3X4), scales=a_scales[m][:], in_=a_bf[m][:].rearrange("p g r t -> p (g r t)"))
 
         def lay(c, k, eng):
             g, h = divmod(k, 2)
-            il = work.tile([P, PIECE, PACK], BF16, tag="w_il", name="w_il", align_bytes=64)
-            w_il[c, k] = il
+            if (c, g) not in w_il:
+                w_il[c, g] = work.tile([P, WIDTH, PACK], BF16, tag="w_il", name="w_il", bufs=4, align_bytes=64)
+            il = w_il[c, g][:, PIECE * h:PIECE * (h + 1), :]
             src = w_raw[c][g][:, :, PIECE * h:PIECE * (h + 1)].rearrange("p j (q i) -> p q j i", i=4)
-            dst = il[:].rearrange("p (q i) j -> p q j i", i=4)
+            dst = il.rearrange("p (q i) j -> p q j i", i=4)
             if eng == "S":
                 nc.scalar.copy(out=dst, in_=src)
             elif eng == "V":
@@ -399,10 +397,9 @@ def tile_gated_adapter_up_s10_kernel(tc, z, scale, base_words, base_scales, doma
             else:
                 nc.gpsimd.tensor_scalar(out=dst, in0=src, scalar1=1.0, scalar2=0.0, op0=ALU.mult, op1=ALU.add)
 
-        def quant_w(c, k):
-            g, h = divmod(k, 2)
-            cols = slice(PIECE * h, PIECE * (h + 1))
-            nc.vector.quantize_mx(out=w_codes[c][:, g, cols].bitcast(E4M3X4), scales=w_scales[c][:, g, cols], in_=w_il[c, k][:].rearrange("p n j -> p (n j)"))
+        def quant_w(c, g, h=None):
+            cols = slice(0, WIDTH) if h is None else slice(PIECE * h, PIECE * (h + 1))
+            nc.vector.quantize_mx(out=w_codes[c][:, g, cols].bitcast(E4M3X4), scales=w_scales[c][:, g, cols], in_=w_il[c, g][:, cols, :].rearrange("p n j -> p (n j)"))
 
         def product(kind, m, c):
             bank = psum.tile([P, WIDTH], F32, tag="bank", name="bank")
@@ -417,19 +414,17 @@ def tile_gated_adapter_up_s10_kernel(tc, z, scale, base_words, base_scales, doma
                 nc.tensor.matmul_mx(out=bank[:], lhsT=a_codes[m][:, g * P:(g + 1) * P].bitcast(E4M3X4), lhsT_scale=a_scales[m][:, g * P:(g + 1) * P], rhs=rhs, rhs_scale=rs, start=(g == 0), stop=(g == GROUPS - 1))
 
         def squash(m, c):
-            t = work.tile([P, WIDTH], F32, tag="tanh", name="tanh", bufs=3)
-            tanh[m, c] = t
+            t = keep.tile([P, WIDTH], F32, name=f"acc{m}{c}")
+            done[m, c] = t
             nc.scalar.activation(out=t[:], in_=banks["g", m, c][:], func=ACT.Tanh, scale=0.5)
 
         def gated(m, c):
-            v = work.tile([P, WIDTH], F32, tag="fold", name="fold", bufs=3)
-            fold[m, c] = v
-            nc.vector.scalar_tensor_tensor(out=v[:], in0=tanh[m, c][:], scalar=1.0, in1=banks["d", m, c][:], op0=ALU.add, op1=ALU.mult)
+            t = done[m, c]
+            nc.vector.scalar_tensor_tensor(out=t[:], in0=t[:], scalar=1.0, in1=banks["d", m, c][:], op0=ALU.add, op1=ALU.mult)
 
         def summed(m, c):
-            y = work.tile([P, WIDTH], F32, tag="done", name="done", bufs=12)
-            done[m, c] = y
-            nc.vector.scalar_tensor_tensor(out=y[:], in0=fold[m, c][:], scalar=0.5, in1=banks["b", m, c][:], op0=ALU.mult, op1=ALU.add)
+            t = done[m, c]
+            nc.vector.scalar_tensor_tensor(out=t[:], in0=t[:], scalar=0.5, in1=banks["b", m, c][:], op0=ALU.mult, op1=ALU.add)
 
         def finish(m, c, eng):
             y = done[m, c]

@@ -17,56 +17,60 @@ P = 128
 PLAN = [
     ("init",),
     ("load_z", 0,),
-    ("turn", 0,),
+    ("load_s",),
+    ("warmup",),
     ("load_w", 0, 0,),
-    ("load_scales", "d", 0, "S",),
-    ("load_scales", "d", 1, "S",),
     ("load_z", 1,),
+    ("load_scales", "d", 0, 0, "S",),
+    ("load_scales", "d", 0, 1, "S",),
+    ("load_scales", "d", 0, 2, "S",),
+    ("load_scales", "d", 0, 3, "S",),
     ("load_w", 0, 1,),
-    ("load_scales", "d", 2, "S",),
-    ("load_scales", "d", 3, "S",),
     ("load_d", 0,),
-    ("turn", 1,),
-    ("load_scales", "b", 0, "Y",),
-    ("gelu", 0,),
+    ("load_scales", "b", 0, 0, "Y",),
+    ("load_scales", "b", 0, 1, "Y",),
+    ("load_scales", "b", 0, 2, "Y",),
+    ("load_scales", "b", 0, 3, "Y",),
     ("load_z", 2,),
-    ("load_scales", "b", 1, "Y",),
-    ("load_b", 0,),
-    ("lay", 0, 1, "V",),
-    ("load_scales", "b", 2, "Y",),
-    ("weigh", 0, "V",),
-    ("gelu", 1,),
     ("load_z", 3,),
-    ("load_scales", "b", 3, "Y",),
-    ("lay", 0, 3, "S",),
-    ("quant_a", 0,),
+    ("load_b", 0,),
     ("load_w", 1, 0,),
     ("load_w", 1, 1,),
     ("load_r", 0,),
     ("load_d", 1,),
-    ("load_b", 1,),
     ("load_z", 4,),
-    ("load_z", 5,),
+    ("load_b", 1,),
     ("load_r", 1,),
     ("load_w", 2, 0,),
     ("load_w", 2, 1,),
+    ("load_scales", "d", 1, 0, "Y",),
+    ("load_scales", "d", 1, 1, "Y",),
+    ("load_scales", "d", 1, 2, "Y",),
+    ("load_scales", "d", 1, 3, "Y",),
+    ("load_scales", "b", 1, 0, "Y",),
+    ("load_scales", "b", 1, 1, "Y",),
+    ("load_scales", "b", 1, 2, "Y",),
+    ("load_scales", "b", 1, 3, "Y",),
     ("load_d", 2,),
-    ("weigh", 1, "V",),
     ("load_b", 2,),
     ("load_r", 2,),
+    ("turn", 0,),
+    ("turn", 1,),
+    ("gelu", 0,),
+    ("lay", 0, 0, "S",),
+    ("weigh", 0, "v",),
+    ("gelu", 1,),
+    ("quant_a", 0,),
     ("product", "d", 0, 0,),
-    ("quant_w", 0, 0, 1,),
     ("lay", 0, 2, "S",),
-    ("lay", 0, 0, "V",),
-    ("load_w", 3, 0,),
-    ("load_w", 3, 1,),
-    ("load_d", 3,),
-    ("load_b", 3,),
-    ("quant_w", 0, 1, 1,),
-    ("load_r", 3,),
-    ("quant_w", 0, 1, 0,),
-    ("quant_a", 1,),
     ("quant_w", 0, 0, 0,),
+    ("lay", 0, 1, "G",),
+    ("lay", 0, 3, "S",),
+    ("weigh", 1, "V",),
+    ("quant_w", 0, 1, 1,),
+    ("quant_w", 0, 1, 0,),
+    ("quant_w", 0, 0, 1,),
+    ("quant_a", 1,),
     ("turn", 2,),
     ("turn", 3,),
     ("product", "g", 0, 0,),
@@ -77,7 +81,7 @@ PLAN = [
     ("gelu", 2,),
     ("gelu", 3,),
     ("lay", 1, 2, "G",),
-    ("lay", 1, 0, "S",),
+    ("lay", 1, 1, "S",),
     ("squash", 0, 0,),
     ("squash", 1, 0,),
     ("weigh", 2, "V",),
@@ -99,7 +103,7 @@ PLAN = [
     ("product", "b", 2, 0,),
     ("product", "b", 3, 0,),
     ("lay", 1, 3, "S",),
-    ("lay", 1, 1, "S",),
+    ("lay", 1, 0, "S",),
     ("squash", 2, 0,),
     ("squash", 3, 0,),
     ("quant_w", 1, 0,),
@@ -159,7 +163,7 @@ PLAN = [
     ("product", "d", 5, 0,),
     ("product", "b", 4, 0,),
     ("product", "b", 5, 0,),
-    ("lay", 2, 0, "S",),
+    ("lay", 2, 1, "S",),
     ("squash", 4, 0,),
     ("squash", 5, 0,),
     ("gated", 4, 0,),
@@ -177,7 +181,7 @@ PLAN = [
     ("product", "b", 4, 1,),
     ("product", "b", 5, 1,),
     ("lay", 2, 3, "S",),
-    ("lay", 2, 1, "S",),
+    ("lay", 2, 0, "S",),
     ("squash", 4, 1,),
     ("squash", 5, 1,),
     ("quant_w", 2, 0,),
@@ -213,7 +217,7 @@ PLAN = [
     ("product", "d", 3, 2,),
     ("product", "b", 2, 2,),
     ("product", "b", 3, 2,),
-    ("lay", 3, 0, "S",),
+    ("lay", 3, 1, "S",),
     ("squash", 2, 2,),
     ("squash", 3, 2,),
     ("gated", 2, 2,),
@@ -231,7 +235,7 @@ PLAN = [
     ("product", "b", 4, 2,),
     ("product", "b", 5, 2,),
     ("lay", 3, 3, "S",),
-    ("lay", 3, 1, "S",),
+    ("lay", 3, 0, "S",),
     ("squash", 4, 2,),
     ("squash", 5, 2,),
     ("quant_w", 3, 0,),
@@ -277,21 +281,25 @@ PLAN = [
     ("finish", 3, 3, "G",),
     ("store", 3, 3,),
     ("product", "g", 4, 3,),
-    ("product", "g", 5, 3,),
     ("product", "d", 4, 3,),
-    ("product", "d", 5, 3,),
     ("product", "b", 4, 3,),
+    ("product", "g", 5, 3,),
+    ("product", "d", 5, 3,),
     ("product", "b", 5, 3,),
     ("squash", 4, 3,),
-    ("squash", 5, 3,),
     ("gated", 4, 3,),
-    ("gated", 5, 3,),
+    ("squash", 5, 3,),
     ("summed", 4, 3,),
     ("finish", 4, 3, "G",),
     ("store", 4, 3,),
-    ("summed", 5, 3,),
-    ("finish", 5, 3, "V",),
-    ("store", 5, 3,),
+    ("gated", 5, 3, 0,),
+    ("gated", 5, 3, 1,),
+    ("summed", 5, 3, 0,),
+    ("summed", 5, 3, 1,),
+    ("finish", 5, 3, "V", 0,),
+    ("store", 5, 3, 0,),
+    ("finish", 5, 3, "V", 1,),
+    ("store", 5, 3, 1,),
 ]
 GROUPS = 2
 PACK = 4
@@ -312,52 +320,66 @@ def tile_gated_adapter_up_s10_kernel(tc, z, scale, base_words, base_scales, doma
         ident = keep.tile([P, P], F32, name="ident")
         warm = keep.tile([P, 1], F32, name="warm")
         scale_col = keep.tile([P, GROUPS, PACK], BF16, name="scale_col")
-        z_raw = [keep.tile([P, K], BF16, name=f"z{m}") for m in range(TILES)]
+        z_pair = [keep.tile([P, 1, K], BF16, name="z0"), keep.tile([P, 1, K], BF16, name="z1"), keep.tile([P, 1, K], BF16, name="z2"), keep.tile([P, 1, K], BF16, name="z3"), keep.tile([P, 2, K], BF16, name="z4")]
+        z_raw = [z_pair[0][:, 0, :], z_pair[1][:, 0, :], z_pair[2][:, 0, :], z_pair[3][:, 0, :], z_pair[4][:, 0, :], z_pair[4][:, 1, :]]
+        LO = [0, WIDTH, 2 * WIDTH]
+        HI = [WIDTH, 2 * WIDTH, N]
         a_codes = [keep.tile([P, GROUPS * P], U32, name=f"ac{m}", align_bytes=64) for m in range(TILES)]
         a_scales = [keep.tile([P, GROUPS * P], U8, name=f"as{m}", align_bytes=64) for m in range(TILES)]
-        w_raw = [[keep.tile([P, PACK, WIDTH], BF16, name=f"w{c}{g}") for g in range(GROUPS)] for c in range(CHUNKS)]
+        w_raw = [[keep.tile([P, PACK, HI[s] - LO[s]], BF16, name=f"w{s}{g}") for g in range(GROUPS)] for s in range(3)]
         w_codes = [keep.tile([P, GROUPS, WIDTH], U32, name=f"wc{c}", align_bytes=64) for c in range(CHUNKS)]
         w_scales = [keep.tile([P, GROUPS, WIDTH], U8, name=f"ws{c}", align_bytes=64) for c in range(CHUNKS)]
-        b_codes = [keep.tile([P, GROUPS, 2 * WIDTH], U8, name=f"bc{c}", align_bytes=64) for c in range(CHUNKS)]
-        d_codes = [keep.tile([P, GROUPS, 4 * WIDTH], U8, name=f"dc{c}", align_bytes=64) for c in range(CHUNKS)]
-        b_planes = keep.tile([P, GROUPS, N], U8, name="b_planes", align_bytes=64)
-        d_planes = keep.tile([P, GROUPS, N], U8, name="d_planes", align_bytes=64)
-        r_raw = [keep.tile([P, TILES, WIDTH], BF16, name=f"r{c}") for c in range(CHUNKS)]
+        b_codes = [keep.tile([P, GROUPS, 2 * (HI[s] - LO[s])], U8, name=f"bc{s}", align_bytes=64) for s in range(3)]
+        d_codes = [keep.tile([P, GROUPS, 4 * (HI[s] - LO[s])], U8, name=f"dc{s}", align_bytes=64) for s in range(3)]
+        b_planes = [keep.tile([P, GROUPS, N // 2], U8, name=f"b_planes{h}", align_bytes=64) for h in range(2)]
+        d_planes = [keep.tile([P, N // 2], U8, name=f"d_planes{h}", align_bytes=64) for h in range(2)]
+        r_raw = [keep.tile([P, TILES, HI[s] - LO[s]], BF16, name=f"r{s}") for s in range(3)]
 
         gel, a_bf, banks, w_il, tanh, fold, done = {}, {}, {}, {}, {}, {}, {}
 
         def load_z(m):
-            nc.sync.dma_start(out=z_raw[m][:], in_=z[m * P:(m + 1) * P, :])
+            t = z_pair[m]
+            n = 1 if m < 4 else 2
+            nc.sync.dma_start(out=t[:], in_=z[m * P:(m + n) * P, :].rearrange("(n p) k -> p n k", p=P))
 
-        def load_w(c, g):
-            nc.sync.dma_start(out=w_raw[c][g][:], in_=w_gate[512 * g:512 * (g + 1), c * WIDTH:(c + 1) * WIDTH].rearrange("(p j) n -> p j n", j=PACK))
+        def load_s():
+            nc.sync.dma_start(out=scale_col[:], in_=scale.rearrange("(g p t) -> p g t", p=P, t=PACK))
 
-        def load_b(c):
-            nc.sync.dma_start(out=b_codes[c][:], in_=base_words[:, :, 2 * WIDTH * c:2 * WIDTH * (c + 1)].rearrange("g p b -> p g b"))
+        def load_w(s, g):
+            nc.sync.dma_start(out=w_raw[s][g][:], in_=w_gate[512 * g:512 * (g + 1), LO[s]:HI[s]].rearrange("(p j) n -> p j n", j=PACK))
 
-        def load_d(c):
-            nc.sync.dma_start(out=d_codes[c][:], in_=domain_words[:, :, WIDTH * c:WIDTH * (c + 1), :].rearrange("g p n t -> p g (n t)"))
+        def load_b(s):
+            nc.sync.dma_start(out=b_codes[s][:], in_=base_words[:, :, 2 * LO[s]:2 * HI[s]].rearrange("g p b -> p g b"))
 
-        def load_r(c):
-            nc.sync.dma_start(out=r_raw[c][:], in_=resid[:, WIDTH * c:WIDTH * (c + 1)].rearrange("(m p) n -> p m n", p=P))
+        def load_d(s):
+            nc.sync.dma_start(out=d_codes[s][:], in_=domain_words[:, :, LO[s]:HI[s], :].rearrange("g p n t -> p g (n t)"))
 
-        def load_scales(kind, q, eng):
-            planes, src = (d_planes, domain_scales) if kind == "d" else (b_planes, base_scales)
-            queue = {"G": nc.gpsimd, "S": nc.scalar, "Y": nc.sync}[eng]
-            queue.dma_start(out=planes[32 * q:32 * q + 4].bitcast(I32), in_=src.bitcast(I32)[:, 4 * q:4 * q + 4, :].rearrange("g r n -> r g n"))
+        def load_r(s):
+            nc.sync.dma_start(out=r_raw[s][:], in_=resid[:, LO[s]:HI[s]].rearrange("(m p) n -> p m n", p=P))
+
+        def load_scales(kind, part, q, eng):
+            a, b = part * N // 8, (part + 1) * N // 8
+            queue = nc.scalar if eng == "S" else nc.sync
+            if kind == "d":
+                queue.dma_start(out=d_planes[part][32 * q + 4:32 * q + 12, :].bitcast(I32), in_=domain_scales.bitcast(I32)[:, 4 * q:4 * q + 4, a:b])
+            else:
+                queue.dma_start(out=b_planes[part][32 * q:32 * q + 4].bitcast(I32), in_=base_scales.bitcast(I32)[:, 4 * q:4 * q + 4, a:b].rearrange("g r n -> r g n"))
 
         def init():
-            nc.scalar.dma_start(out=scale_col[:], in_=scale.rearrange("(g p t) -> p g t", p=P, t=PACK))
+            nc.vector.memset(d_planes[0][:].bitcast(I32), 0)
             nc.vector.memset(warm[:], 0.0)
-            nc.scalar.activation(out=warm[:], in_=warm[:], func=ACT.Gelu_apprx_tanh)
-            nc.vector.memset(d_planes[:].rearrange("p g n -> p (g n)").bitcast(I32), 0)
-            nc.vector.memset(b_planes[:].rearrange("p g n -> p (g n)").bitcast(I32), 0)
+            nc.vector.memset(b_planes[0][:].rearrange("p g n -> p (g n)").bitcast(I32), 0)
+            nc.vector.memset(d_planes[1][:].bitcast(I32), 0)
+            nc.vector.memset(b_planes[1][:].rearrange("p g n -> p (g n)").bitcast(I32), 0)
             make_identity(nc, ident[:])
+
+        def warmup():
+            nc.scalar.activation(out=warm[:], in_=warm[:], func=ACT.Gelu_apprx_tanh)
 
         def turn(m):
             bank = psum.tile([P, GROUPS, 2, P], F32, tag="bank", name="bank")
             banks["a", m] = bank
-            words = z_raw[m][:].bitcast(F32)
+            words = z_raw[m].bitcast(F32)
             for g in range(GROUPS):
                 for u in range(2):
                     nc.tensor.transpose(bank[:, g, u, :], words[:, 256 * g + u:256 * (g + 1):2], ident[:])
@@ -374,7 +396,7 @@ def tile_gated_adapter_up_s10_kernel(tc, z, scale, base_words, base_scales, doma
         def weigh(m, eng="V"):
             a_bf[m] = work.tile([P, GROUPS, P, PACK], BF16, tag="a_bf", name="a_bf", bufs=6, align_bytes=64)
             e = nc.gpsimd if eng == "G" else nc.vector
-            if eng == "G":
+            if eng in "Gv":
                 for g in range(GROUPS):
                     e.tensor_tensor(out=a_bf[m][:, g], in0=gel[m][:, g], in1=scale_col[:, g, :].unsqueeze(1).to_broadcast([P, P, PACK]), op=ALU.mult)
             else:
@@ -388,7 +410,8 @@ def tile_gated_adapter_up_s10_kernel(tc, z, scale, base_words, base_scales, doma
             if (c, g) not in w_il:
                 w_il[c, g] = work.tile([P, WIDTH, PACK], BF16, tag="w_il", name="w_il", bufs=4, align_bytes=64)
             il = w_il[c, g][:, PIECE * h:PIECE * (h + 1), :]
-            src = w_raw[c][g][:, :, PIECE * h:PIECE * (h + 1)].rearrange("p j (q i) -> p q j i", i=4)
+            s, o = (c, 0) if c < 2 else (2, WIDTH * (c - 2))
+            src = w_raw[s][g][:, :, o + PIECE * h:o + PIECE * (h + 1)].rearrange("p j (q i) -> p q j i", i=4)
             dst = il.rearrange("p (q i) j -> p q j i", i=4)
             if eng == "S":
                 nc.scalar.copy(out=dst, in_=src)
@@ -404,13 +427,15 @@ def tile_gated_adapter_up_s10_kernel(tc, z, scale, base_words, base_scales, doma
         def product(kind, m, c):
             bank = psum.tile([P, WIDTH], F32, tag="bank", name="bank")
             banks[kind, m, c] = bank
+            s, o = (c, 0) if c < 2 else (2, WIDTH * (c - 2))
             for g in range(GROUPS):
                 if kind == "g":
                     rhs, rs = w_codes[c][:, g, :].bitcast(E4M3X4), w_scales[c][:, g, :]
                 elif kind == "d":
-                    rhs, rs = d_codes[c][:, g, :].bitcast(E4M3X4), d_planes[:, g, WIDTH * c:WIDTH * (c + 1)]
+                    k = 4 + 4 * g
+                    rhs, rs = d_codes[s][:, g, 4 * o:4 * (o + WIDTH)].bitcast(E4M3X4), d_planes[c // 2][k:P, WIDTH * (c % 2):WIDTH * (c % 2 + 1)]
                 else:
-                    rhs, rs = b_codes[c][:, g, :].bitcast(E2M1X4), b_planes[:, g, WIDTH * c:WIDTH * (c + 1)]
+                    rhs, rs = b_codes[s][:, g, 2 * o:2 * (o + WIDTH)].bitcast(E2M1X4), b_planes[c // 2][:, g, WIDTH * (c % 2):WIDTH * (c % 2 + 1)]
                 nc.tensor.matmul_mx(out=bank[:], lhsT=a_codes[m][:, g * P:(g + 1) * P].bitcast(E4M3X4), lhsT_scale=a_scales[m][:, g * P:(g + 1) * P], rhs=rhs, rhs_scale=rs, start=(g == 0), stop=(g == GROUPS - 1))
 
         def squash(m, c):
@@ -418,22 +443,36 @@ def tile_gated_adapter_up_s10_kernel(tc, z, scale, base_words, base_scales, doma
             done[m, c] = t
             nc.scalar.activation(out=t[:], in_=banks["g", m, c][:], func=ACT.Tanh, scale=0.5)
 
-        def gated(m, c):
-            t = done[m, c]
-            nc.vector.scalar_tensor_tensor(out=t[:], in0=t[:], scalar=1.0, in1=banks["d", m, c][:], op0=ALU.add, op1=ALU.mult)
+        def gated(m, c, h=None):
+            cols = slice(0, WIDTH) if h is None else slice(PIECE * h, PIECE * (h + 1))
+            t = done[m, c][:, cols]
+            nc.vector.scalar_tensor_tensor(out=t, in0=t, scalar=1.0, in1=banks["d", m, c][:, cols], op0=ALU.add, op1=ALU.mult)
 
-        def summed(m, c):
-            t = done[m, c]
-            nc.vector.scalar_tensor_tensor(out=t[:], in0=t[:], scalar=0.5, in1=banks["b", m, c][:], op0=ALU.mult, op1=ALU.add)
+        def summed(m, c, h=None):
+            cols = slice(0, WIDTH) if h is None else slice(PIECE * h, PIECE * (h + 1))
+            t = done[m, c][:, cols]
+            nc.vector.scalar_tensor_tensor(out=t, in0=t, scalar=0.5, in1=banks["b", m, c][:, cols], op0=ALU.mult, op1=ALU.add)
 
-        def finish(m, c, eng):
-            y = done[m, c]
+        def early(m, c):
+            t = done[m, c]
+            s, o = (c, 0) if c < 2 else (2, WIDTH * (c - 2))
+            nc.vector.scalar_tensor_tensor(out=t[:], in0=t[:], scalar=0.5, in1=r_raw[s][:, m, o:o + WIDTH], op0=ALU.mult, op1=ALU.add)
+
+        def closing(m, c):
+            t = done[m, c]
+            nc.vector.tensor_tensor(out=t[:], in0=t[:], in1=banks["b", m, c][:], op=ALU.add)
+
+        def finish(m, c, eng, h=None):
+            cols = slice(0, WIDTH) if h is None else slice(PIECE * h, PIECE * (h + 1))
+            y = done[m, c][:, cols]
             e = nc.gpsimd if eng == "G" else nc.vector
-            e.tensor_tensor(out=y[:], in0=y[:], in1=r_raw[c][:, m, :], op=ALU.add)
+            s, o = (c, 0) if c < 2 else (2, WIDTH * (c - 2))
+            e.tensor_tensor(out=y, in0=y, in1=r_raw[s][:, m, o:o + WIDTH][:, cols], op=ALU.add)
 
-        def store(m, c):
-            nc.sync.dma_start(out=out[m * P:(m + 1) * P, c * WIDTH:(c + 1) * WIDTH], in_=done[m, c][:])
+        def store(m, c, h=None):
+            cols = slice(0, WIDTH) if h is None else slice(PIECE * h, PIECE * (h + 1))
+            nc.sync.dma_start(out=out[m * P:(m + 1) * P, c * WIDTH:(c + 1) * WIDTH][:, cols], in_=done[m, c][:, cols])
 
-        ops = dict(init=init, load_scales=load_scales, load_z=load_z, load_w=load_w, load_b=load_b, load_d=load_d, load_r=load_r, gelu=gelu, turn=turn, weigh=weigh, quant_a=quant_a, lay=lay, quant_w=quant_w, product=product, squash=squash, gated=gated, summed=summed, finish=finish, store=store)
+        ops = dict(early=early, closing=closing, init=init, load_s=load_s, warmup=warmup, load_scales=load_scales, load_z=load_z, load_w=load_w, load_b=load_b, load_d=load_d, load_r=load_r, gelu=gelu, turn=turn, weigh=weigh, quant_a=quant_a, lay=lay, quant_w=quant_w, product=product, squash=squash, gated=gated, summed=summed, finish=finish, store=store)
         for step in PLAN:
             ops[step[0]](*step[1:])

@@ -1,9 +1,11 @@
 from contextlib import ExitStack
+
 import concourse.mybir as mybir
 from concourse.masks import make_identity
 
 M, K, N = 768, 1024, 2048
 FLOPS = 3 * 2 * M * K * N
+
 F32 = mybir.dt.float32
 BF16 = mybir.dt.bfloat16
 U32 = mybir.dt.uint32
@@ -13,303 +15,37 @@ E4M3X4 = mybir.dt.float8_e4m3fn_x4
 E2M1X4 = mybir.dt.float4_e2m1fn_x4
 ACT = mybir.ActivationFunctionType
 ALU = mybir.AluOpType
+
 P = 128
-PLAN = [
-    ("init",),
-    ("load_z", 0,),
-    ("load_s",),
-    ("warmup",),
-    ("load_w", 0, 0,),
-    ("load_z", 1,),
-    ("load_scales", "d", 0, 0, "S",),
-    ("load_scales", "d", 0, 1, "S",),
-    ("load_scales", "d", 0, 2, "S",),
-    ("load_scales", "d", 0, 3, "S",),
-    ("load_w", 0, 1,),
-    ("load_d", 0,),
-    ("load_scales", "b", 0, 0, "Y",),
-    ("load_scales", "b", 0, 1, "Y",),
-    ("load_scales", "b", 0, 2, "Y",),
-    ("load_scales", "b", 0, 3, "Y",),
-    ("load_z", 2,),
-    ("load_z", 3,),
-    ("load_b", 0,),
-    ("load_w", 1, 0,),
-    ("load_w", 1, 1,),
-    ("load_r", 0,),
-    ("load_d", 1,),
-    ("load_z", 4,),
-    ("load_b", 1,),
-    ("load_r", 1,),
-    ("load_w", 2, 0,),
-    ("load_w", 2, 1,),
-    ("load_scales", "d", 1, 0, "Y",),
-    ("load_scales", "d", 1, 1, "Y",),
-    ("load_scales", "d", 1, 2, "Y",),
-    ("load_scales", "d", 1, 3, "Y",),
-    ("load_scales", "b", 1, 0, "Y",),
-    ("load_scales", "b", 1, 1, "Y",),
-    ("load_scales", "b", 1, 2, "Y",),
-    ("load_scales", "b", 1, 3, "Y",),
-    ("load_d", 2,),
-    ("load_b", 2,),
-    ("load_r", 2,),
-    ("turn", 0,),
-    ("turn", 1,),
-    ("gelu", 0,),
-    ("lay", 0, 0, "S",),
-    ("weigh", 0, "v",),
-    ("gelu", 1,),
-    ("quant_a", 0,),
-    ("product", "d", 0, 0,),
-    ("lay", 0, 2, "S",),
-    ("quant_w", 0, 0, 0,),
-    ("lay", 0, 1, "G",),
-    ("lay", 0, 3, "S",),
-    ("weigh", 1, "V",),
-    ("quant_w", 0, 1, 1,),
-    ("quant_w", 0, 1, 0,),
-    ("quant_w", 0, 0, 1,),
-    ("quant_a", 1,),
-    ("turn", 2,),
-    ("turn", 3,),
-    ("product", "g", 0, 0,),
-    ("product", "g", 1, 0,),
-    ("product", "d", 1, 0,),
-    ("product", "b", 0, 0,),
-    ("product", "b", 1, 0,),
-    ("gelu", 2,),
-    ("gelu", 3,),
-    ("lay", 1, 2, "G",),
-    ("lay", 1, 1, "S",),
-    ("squash", 0, 0,),
-    ("squash", 1, 0,),
-    ("weigh", 2, "V",),
-    ("weigh", 3, "V",),
-    ("quant_a", 2,),
-    ("quant_a", 3,),
-    ("gated", 0, 0,),
-    ("gated", 1, 0,),
-    ("summed", 0, 0,),
-    ("finish", 0, 0, "G",),
-    ("store", 0, 0,),
-    ("summed", 1, 0,),
-    ("finish", 1, 0, "G",),
-    ("store", 1, 0,),
-    ("product", "g", 2, 0,),
-    ("product", "g", 3, 0,),
-    ("product", "d", 2, 0,),
-    ("product", "d", 3, 0,),
-    ("product", "b", 2, 0,),
-    ("product", "b", 3, 0,),
-    ("lay", 1, 3, "S",),
-    ("lay", 1, 0, "S",),
-    ("squash", 2, 0,),
-    ("squash", 3, 0,),
-    ("quant_w", 1, 0,),
-    ("quant_w", 1, 1,),
-    ("gated", 2, 0,),
-    ("gated", 3, 0,),
-    ("summed", 2, 0,),
-    ("finish", 2, 0, "G",),
-    ("store", 2, 0,),
-    ("summed", 3, 0,),
-    ("finish", 3, 0, "G",),
-    ("store", 3, 0,),
-    ("turn", 4,),
-    ("turn", 5,),
-    ("product", "g", 0, 1,),
-    ("product", "g", 1, 1,),
-    ("product", "d", 0, 1,),
-    ("product", "d", 1, 1,),
-    ("product", "b", 0, 1,),
-    ("product", "b", 1, 1,),
-    ("gelu", 4,),
-    ("gelu", 5,),
-    ("squash", 0, 1,),
-    ("squash", 1, 1,),
-    ("weigh", 4, "V",),
-    ("weigh", 5, "V",),
-    ("quant_a", 4,),
-    ("quant_a", 5,),
-    ("gated", 0, 1,),
-    ("gated", 1, 1,),
-    ("summed", 0, 1,),
-    ("finish", 0, 1, "G",),
-    ("store", 0, 1,),
-    ("summed", 1, 1,),
-    ("finish", 1, 1, "G",),
-    ("store", 1, 1,),
-    ("product", "g", 2, 1,),
-    ("product", "g", 3, 1,),
-    ("product", "d", 2, 1,),
-    ("product", "d", 3, 1,),
-    ("product", "b", 2, 1,),
-    ("product", "b", 3, 1,),
-    ("lay", 2, 2, "S",),
-    ("squash", 2, 1,),
-    ("squash", 3, 1,),
-    ("gated", 2, 1,),
-    ("gated", 3, 1,),
-    ("summed", 2, 1,),
-    ("finish", 2, 1, "G",),
-    ("store", 2, 1,),
-    ("summed", 3, 1,),
-    ("finish", 3, 1, "G",),
-    ("store", 3, 1,),
-    ("product", "g", 4, 0,),
-    ("product", "g", 5, 0,),
-    ("product", "d", 4, 0,),
-    ("product", "d", 5, 0,),
-    ("product", "b", 4, 0,),
-    ("product", "b", 5, 0,),
-    ("lay", 2, 1, "S",),
-    ("squash", 4, 0,),
-    ("squash", 5, 0,),
-    ("gated", 4, 0,),
-    ("gated", 5, 0,),
-    ("summed", 4, 0,),
-    ("finish", 4, 0, "G",),
-    ("store", 4, 0,),
-    ("summed", 5, 0,),
-    ("finish", 5, 0, "G",),
-    ("store", 5, 0,),
-    ("product", "g", 4, 1,),
-    ("product", "g", 5, 1,),
-    ("product", "d", 4, 1,),
-    ("product", "d", 5, 1,),
-    ("product", "b", 4, 1,),
-    ("product", "b", 5, 1,),
-    ("lay", 2, 3, "S",),
-    ("lay", 2, 0, "S",),
-    ("squash", 4, 1,),
-    ("squash", 5, 1,),
-    ("quant_w", 2, 0,),
-    ("quant_w", 2, 1,),
-    ("gated", 4, 1,),
-    ("gated", 5, 1,),
-    ("summed", 4, 1,),
-    ("finish", 4, 1, "G",),
-    ("store", 4, 1,),
-    ("summed", 5, 1,),
-    ("finish", 5, 1, "G",),
-    ("store", 5, 1,),
-    ("product", "g", 0, 2,),
-    ("product", "g", 1, 2,),
-    ("product", "d", 0, 2,),
-    ("product", "d", 1, 2,),
-    ("product", "b", 0, 2,),
-    ("product", "b", 1, 2,),
-    ("lay", 3, 2, "S",),
-    ("squash", 0, 2,),
-    ("squash", 1, 2,),
-    ("gated", 0, 2,),
-    ("gated", 1, 2,),
-    ("summed", 0, 2,),
-    ("finish", 0, 2, "G",),
-    ("store", 0, 2,),
-    ("summed", 1, 2,),
-    ("finish", 1, 2, "G",),
-    ("store", 1, 2,),
-    ("product", "g", 2, 2,),
-    ("product", "g", 3, 2,),
-    ("product", "d", 2, 2,),
-    ("product", "d", 3, 2,),
-    ("product", "b", 2, 2,),
-    ("product", "b", 3, 2,),
-    ("lay", 3, 1, "S",),
-    ("squash", 2, 2,),
-    ("squash", 3, 2,),
-    ("gated", 2, 2,),
-    ("gated", 3, 2,),
-    ("summed", 2, 2,),
-    ("finish", 2, 2, "G",),
-    ("store", 2, 2,),
-    ("summed", 3, 2,),
-    ("finish", 3, 2, "G",),
-    ("store", 3, 2,),
-    ("product", "g", 4, 2,),
-    ("product", "g", 5, 2,),
-    ("product", "d", 4, 2,),
-    ("product", "d", 5, 2,),
-    ("product", "b", 4, 2,),
-    ("product", "b", 5, 2,),
-    ("lay", 3, 3, "S",),
-    ("lay", 3, 0, "S",),
-    ("squash", 4, 2,),
-    ("squash", 5, 2,),
-    ("quant_w", 3, 0,),
-    ("quant_w", 3, 1,),
-    ("gated", 4, 2,),
-    ("gated", 5, 2,),
-    ("summed", 4, 2,),
-    ("finish", 4, 2, "G",),
-    ("store", 4, 2,),
-    ("summed", 5, 2,),
-    ("finish", 5, 2, "G",),
-    ("store", 5, 2,),
-    ("product", "g", 0, 3,),
-    ("product", "g", 1, 3,),
-    ("product", "d", 0, 3,),
-    ("product", "d", 1, 3,),
-    ("product", "b", 0, 3,),
-    ("product", "b", 1, 3,),
-    ("squash", 0, 3,),
-    ("squash", 1, 3,),
-    ("gated", 0, 3,),
-    ("gated", 1, 3,),
-    ("summed", 0, 3,),
-    ("finish", 0, 3, "G",),
-    ("store", 0, 3,),
-    ("summed", 1, 3,),
-    ("finish", 1, 3, "G",),
-    ("store", 1, 3,),
-    ("product", "g", 2, 3,),
-    ("product", "g", 3, 3,),
-    ("product", "d", 2, 3,),
-    ("product", "d", 3, 3,),
-    ("product", "b", 2, 3,),
-    ("product", "b", 3, 3,),
-    ("squash", 2, 3,),
-    ("squash", 3, 3,),
-    ("gated", 2, 3,),
-    ("gated", 3, 3,),
-    ("summed", 2, 3,),
-    ("finish", 2, 3, "G",),
-    ("store", 2, 3,),
-    ("summed", 3, 3,),
-    ("finish", 3, 3, "G",),
-    ("store", 3, 3,),
-    ("product", "g", 4, 3,),
-    ("product", "d", 4, 3,),
-    ("product", "b", 4, 3,),
-    ("product", "g", 5, 3,),
-    ("product", "d", 5, 3,),
-    ("product", "b", 5, 3,),
-    ("squash", 4, 3,),
-    ("gated", 4, 3,),
-    ("squash", 5, 3,),
-    ("summed", 4, 3,),
-    ("finish", 4, 3, "G",),
-    ("store", 4, 3,),
-    ("gated", 5, 3, 0,),
-    ("gated", 5, 3, 1,),
-    ("summed", 5, 3, 0,),
-    ("summed", 5, 3, 1,),
-    ("finish", 5, 3, "V", 0,),
-    ("store", 5, 3, 0,),
-    ("finish", 5, 3, "V", 1,),
-    ("store", 5, 3, 1,),
-]
-GROUPS = 2
 PACK = 4
-TILES = 6
-CHUNKS = 4
+GROUPS = 2
+GROUP_K = P * PACK
+TILES = M // P
 WIDTH = 512
-PIECE = 256
+CHUNKS = N // WIDTH
+HALF = WIDTH // 2
+HALVES = (0, 1)
+PART = N // 2
+PARTS = range(N // PART)
+QUADRANTS = 4
+QUADRANT = P // QUADRANTS
+ROWS = 4
+
+SPANS = [(0, WIDTH), (WIDTH, 2 * WIDTH), (2 * WIDTH, N)]
 
 
-def tile_gated_adapter_up_s10_kernel(tc, z, scale, base_words, base_scales, domain_words, domain_scales, w_gate, resid, out):
+def locate(c):
+    s = min(c, len(SPANS) - 1)
+    return s, WIDTH * c - SPANS[s][0]
+
+
+def columns(half):
+    return slice(0, WIDTH) if half is None else slice(HALF * half, HALF * (half + 1))
+
+
+def tile_gated_adapter_up_s10_kernel(
+    tc, z, scale, base_words, base_scales, domain_words, domain_scales, w_gate, resid, out
+):
     nc = tc.nc
     with ExitStack() as ctx:
         keep = ctx.enter_context(tc.tile_pool(name="keep", bufs=1))
@@ -318,161 +54,317 @@ def tile_gated_adapter_up_s10_kernel(tc, z, scale, base_words, base_scales, doma
         ctx.enter_context(tc.manual_schedule())
 
         ident = keep.tile([P, P], F32, name="ident")
-        warm = keep.tile([P, 1], F32, name="warm")
-        scale_col = keep.tile([P, GROUPS, PACK], BF16, name="scale_col")
-        z_pair = [keep.tile([P, 1, K], BF16, name="z0"), keep.tile([P, 1, K], BF16, name="z1"), keep.tile([P, 1, K], BF16, name="z2"), keep.tile([P, 1, K], BF16, name="z3"), keep.tile([P, 2, K], BF16, name="z4")]
-        z_raw = [z_pair[0][:, 0, :], z_pair[1][:, 0, :], z_pair[2][:, 0, :], z_pair[3][:, 0, :], z_pair[4][:, 0, :], z_pair[4][:, 1, :]]
-        LO = [0, WIDTH, 2 * WIDTH]
-        HI = [WIDTH, 2 * WIDTH, N]
+        dummy = keep.tile([P, 1], F32, name="dummy")
+        scale_k = keep.tile([P, GROUPS, PACK], BF16, name="scale_k")
+        z_one = [keep.tile([P, 1, K], BF16, name=f"z{m}") for m in range(TILES - 2)]
+        z_two = keep.tile([P, 2, K], BF16, name="z4")
+        z_rows = [t[:, 0, :] for t in z_one] + [z_two[:, i, :] for i in range(2)]
         a_codes = [keep.tile([P, GROUPS * P], U32, name=f"ac{m}", align_bytes=64) for m in range(TILES)]
         a_scales = [keep.tile([P, GROUPS * P], U8, name=f"as{m}", align_bytes=64) for m in range(TILES)]
-        w_raw = [[keep.tile([P, PACK, HI[s] - LO[s]], BF16, name=f"w{s}{g}") for g in range(GROUPS)] for s in range(3)]
+        w_raw = [
+            [keep.tile([P, PACK, hi - lo], BF16, name=f"w{s}{g}") for g in range(GROUPS)]
+            for s, (lo, hi) in enumerate(SPANS)
+        ]
         w_codes = [keep.tile([P, GROUPS, WIDTH], U32, name=f"wc{c}", align_bytes=64) for c in range(CHUNKS)]
         w_scales = [keep.tile([P, GROUPS, WIDTH], U8, name=f"ws{c}", align_bytes=64) for c in range(CHUNKS)]
-        b_codes = [keep.tile([P, GROUPS, 2 * (HI[s] - LO[s])], U8, name=f"bc{s}", align_bytes=64) for s in range(3)]
-        d_codes = [keep.tile([P, GROUPS, 4 * (HI[s] - LO[s])], U8, name=f"dc{s}", align_bytes=64) for s in range(3)]
-        b_planes = [keep.tile([P, GROUPS, N // 2], U8, name=f"b_planes{h}", align_bytes=64) for h in range(2)]
-        d_planes = [keep.tile([P, N // 2], U8, name=f"d_planes{h}", align_bytes=64) for h in range(2)]
-        r_raw = [keep.tile([P, TILES, HI[s] - LO[s]], BF16, name=f"r{s}") for s in range(3)]
+        b_codes = [
+            keep.tile([P, GROUPS, 2 * (hi - lo)], U8, name=f"bc{s}", align_bytes=64) for s, (lo, hi) in enumerate(SPANS)
+        ]
+        d_codes = [
+            keep.tile([P, GROUPS, 4 * (hi - lo)], U8, name=f"dc{s}", align_bytes=64) for s, (lo, hi) in enumerate(SPANS)
+        ]
+        b_scales = [keep.tile([P, GROUPS, PART], U8, name=f"bs{h}", align_bytes=64) for h in PARTS]
+        d_scales = [keep.tile([P, PART], U8, name=f"ds{h}", align_bytes=64) for h in PARTS]
+        r_rows = [keep.tile([P, TILES, hi - lo], BF16, name=f"r{s}") for s, (lo, hi) in enumerate(SPANS)]
 
-        gel, a_bf, banks, w_il, tanh, fold, done = {}, {}, {}, {}, {}, {}, {}
+        turned, gelu_z, a_bf, w_grouped, banks, result = {}, {}, {}, {}, {}, {}
+
 
         def load_z(m):
-            t = z_pair[m]
-            n = 1 if m < 4 else 2
-            nc.sync.dma_start(out=t[:], in_=z[m * P:(m + n) * P, :].rearrange("(n p) k -> p n k", p=P))
+            nc.sync.dma_start(out=z_one[m][:], in_=z[m * P : (m + 1) * P, :].rearrange("(n p) k -> p n k", p=P))
 
-        def load_s():
-            nc.sync.dma_start(out=scale_col[:], in_=scale.rearrange("(g p t) -> p g t", p=P, t=PACK))
+        def load_last_z():
+            nc.sync.dma_start(out=z_two[:], in_=z[(TILES - 2) * P :, :].rearrange("(n p) k -> p n k", p=P))
+
+        def load_scale():
+            nc.sync.dma_start(out=scale_k[:], in_=scale.rearrange("(g p t) -> p g t", p=P, t=PACK))
 
         def load_w(s, g):
-            nc.sync.dma_start(out=w_raw[s][g][:], in_=w_gate[512 * g:512 * (g + 1), LO[s]:HI[s]].rearrange("(p j) n -> p j n", j=PACK))
+            lo, hi = SPANS[s]
+            rows = w_gate[GROUP_K * g : GROUP_K * (g + 1), lo:hi]
+            nc.sync.dma_start(out=w_raw[s][g][:], in_=rows.rearrange("(p t) n -> p t n", t=PACK))
 
         def load_b(s):
-            nc.sync.dma_start(out=b_codes[s][:], in_=base_words[:, :, 2 * LO[s]:2 * HI[s]].rearrange("g p b -> p g b"))
+            lo, hi = SPANS[s]
+            nc.sync.dma_start(out=b_codes[s][:], in_=base_words[:, :, 2 * lo : 2 * hi].rearrange("g p n -> p g n"))
 
         def load_d(s):
-            nc.sync.dma_start(out=d_codes[s][:], in_=domain_words[:, :, LO[s]:HI[s], :].rearrange("g p n t -> p g (n t)"))
+            lo, hi = SPANS[s]
+            nc.sync.dma_start(out=d_codes[s][:], in_=domain_words[:, :, lo:hi, :].rearrange("g p n t -> p g (n t)"))
 
         def load_r(s):
-            nc.sync.dma_start(out=r_raw[s][:], in_=resid[:, LO[s]:HI[s]].rearrange("(m p) n -> p m n", p=P))
+            lo, hi = SPANS[s]
+            nc.sync.dma_start(out=r_rows[s][:], in_=resid[:, lo:hi].rearrange("(m p) n -> p m n", p=P))
 
-        def load_scales(kind, part, q, eng):
-            a, b = part * N // 8, (part + 1) * N // 8
-            queue = nc.scalar if eng == "S" else nc.sync
-            if kind == "d":
-                queue.dma_start(out=d_planes[part][32 * q + 4:32 * q + 12, :].bitcast(I32), in_=domain_scales.bitcast(I32)[:, 4 * q:4 * q + 4, a:b])
-            else:
-                queue.dma_start(out=b_planes[part][32 * q:32 * q + 4].bitcast(I32), in_=base_scales.bitcast(I32)[:, 4 * q:4 * q + 4, a:b].rearrange("g r n -> r g n"))
+        def load_b_scales(h):
+            int32s = slice(h * PART // 4, (h + 1) * PART // 4)
+            for quad in range(QUADRANTS):
+                first = QUADRANT * quad
+                nc.sync.dma_start(
+                    out=b_scales[h][first : first + ROWS].bitcast(I32),
+                    in_=base_scales.bitcast(I32)[:, ROWS * quad : ROWS * (quad + 1), int32s].rearrange("g r n -> r g n"),
+                )
 
-        def init():
-            nc.vector.memset(d_planes[0][:].bitcast(I32), 0)
-            nc.vector.memset(warm[:], 0.0)
-            nc.vector.memset(b_planes[0][:].rearrange("p g n -> p (g n)").bitcast(I32), 0)
-            nc.vector.memset(d_planes[1][:].bitcast(I32), 0)
-            nc.vector.memset(b_planes[1][:].rearrange("p g n -> p (g n)").bitcast(I32), 0)
-            make_identity(nc, ident[:])
+        def load_d_scales(h):
+            int32s = slice(h * PART // 4, (h + 1) * PART // 4)
+            for quad in range(QUADRANTS):
+                first = QUADRANT * quad + ROWS
+                nc.sync.dma_start(
+                    out=d_scales[h][first : first + GROUPS * ROWS, :].bitcast(I32),
+                    in_=domain_scales.bitcast(I32)[:, ROWS * quad : ROWS * (quad + 1), int32s],
+                )
 
-        def warmup():
-            nc.scalar.activation(out=warm[:], in_=warm[:], func=ACT.Gelu_apprx_tanh)
 
         def turn(m):
-            bank = psum.tile([P, GROUPS, 2, P], F32, tag="bank", name="bank")
-            banks["a", m] = bank
-            words = z_raw[m].bitcast(F32)
+            turned[m] = psum.tile([P, GROUPS, 2, P], F32, tag="bank", name="bank")
+            pairs = z_rows[m].bitcast(F32)
+            count = GROUP_K // 2
             for g in range(GROUPS):
                 for u in range(2):
-                    nc.tensor.transpose(bank[:, g, u, :], words[:, 256 * g + u:256 * (g + 1):2], ident[:])
+                    nc.tensor.transpose(turned[m][:, g, u, :], pairs[:, count * g + u : count * (g + 1) : 2], ident[:])
 
         def gelu(m):
-            gel[m] = work.tile([P, GROUPS, P, PACK], F32, tag="gel", name="gel", bufs=6)
-            pairs = banks["a", m][:].rearrange("p g u r -> p (g u r)").bitcast(BF16)
+            gelu_z[m] = work.tile([P, GROUPS, P, PACK], F32, tag="gelu", name="gelu", bufs=TILES)
+            pairs = turned[m][:].rearrange("p g u r -> p (g u r)").bitcast(BF16)
             for g in range(GROUPS):
                 nc.scalar.activation(
-                    out=gel[m][:, g].rearrange("p r (u e) -> p r u e", u=2),
-                    in_=pairs[:, 512 * g:512 * (g + 1)].rearrange("p (u r e) -> p r u e", u=2, e=2),
-                    func=ACT.Gelu_apprx_tanh)
+                    out=gelu_z[m][:, g].rearrange("p r (u e) -> p r u e", u=2),
+                    in_=pairs[:, GROUP_K * g : GROUP_K * (g + 1)].rearrange("p (u r e) -> p r u e", u=2, e=2),
+                    func=ACT.Gelu_apprx_tanh,
+                )
 
-        def weigh(m, eng="V"):
-            a_bf[m] = work.tile([P, GROUPS, P, PACK], BF16, tag="a_bf", name="a_bf", bufs=6, align_bytes=64)
-            e = nc.gpsimd if eng == "G" else nc.vector
-            if eng in "Gv":
+        def multiply_scale(m, by_group=False):
+            a_bf[m] = work.tile([P, GROUPS, P, PACK], BF16, tag="a_bf", name="a_bf", bufs=TILES, align_bytes=64)
+            if by_group:
                 for g in range(GROUPS):
-                    e.tensor_tensor(out=a_bf[m][:, g], in0=gel[m][:, g], in1=scale_col[:, g, :].unsqueeze(1).to_broadcast([P, P, PACK]), op=ALU.mult)
+                    factor = scale_k[:, g, :].unsqueeze(1).to_broadcast([P, P, PACK])
+                    nc.vector.tensor_tensor(out=a_bf[m][:, g], in0=gelu_z[m][:, g], in1=factor, op=ALU.mult)
             else:
-                e.tensor_tensor(out=a_bf[m][:], in0=gel[m][:], in1=scale_col[:].unsqueeze(2).to_broadcast([P, GROUPS, P, PACK]), op=ALU.mult)
+                factor = scale_k[:].unsqueeze(2).to_broadcast([P, GROUPS, P, PACK])
+                nc.vector.tensor_tensor(out=a_bf[m][:], in0=gelu_z[m][:], in1=factor, op=ALU.mult)
 
-        def quant_a(m):
-            nc.vector.quantize_mx(out=a_codes[m][:].bitcast(E4M3X4), scales=a_scales[m][:], in_=a_bf[m][:].rearrange("p g r t -> p (g r t)"))
+        def quantize_a(m):
+            nc.vector.quantize_mx(
+                out=a_codes[m][:].bitcast(E4M3X4),
+                scales=a_scales[m][:],
+                in_=a_bf[m][:].rearrange("p g r t -> p (g r t)"),
+            )
 
-        def lay(c, k, eng):
-            g, h = divmod(k, 2)
-            if (c, g) not in w_il:
-                w_il[c, g] = work.tile([P, WIDTH, PACK], BF16, tag="w_il", name="w_il", bufs=4, align_bytes=64)
-            il = w_il[c, g][:, PIECE * h:PIECE * (h + 1), :]
-            s, o = (c, 0) if c < 2 else (2, WIDTH * (c - 2))
-            src = w_raw[s][g][:, :, o + PIECE * h:o + PIECE * (h + 1)].rearrange("p j (q i) -> p q j i", i=4)
-            dst = il.rearrange("p (q i) j -> p q j i", i=4)
-            if eng == "S":
+        def interleave_w(c, g, half, engine):
+            if (c, g) not in w_grouped:
+                w_grouped[c, g] = work.tile(
+                    [P, WIDTH, PACK], BF16, tag="w_grouped", name="w_grouped", bufs=2 * GROUPS, align_bytes=64
+                )
+            s, first = locate(c)
+            cols = slice(first + HALF * half, first + HALF * (half + 1))
+            src = w_raw[s][g][:, :, cols].rearrange("p t (q i) -> p q t i", i=4)
+            dst = w_grouped[c, g][:, columns(half), :].rearrange("p (q i) t -> p q t i", i=4)
+            if engine == "scalar":
                 nc.scalar.copy(out=dst, in_=src)
-            elif eng == "V":
+            elif engine == "vector":
                 nc.vector.tensor_copy(out=dst, in_=src)
             else:
                 nc.gpsimd.tensor_scalar(out=dst, in0=src, scalar1=1.0, scalar2=0.0, op0=ALU.mult, op1=ALU.add)
 
-        def quant_w(c, g, h=None):
-            cols = slice(0, WIDTH) if h is None else slice(PIECE * h, PIECE * (h + 1))
-            nc.vector.quantize_mx(out=w_codes[c][:, g, cols].bitcast(E4M3X4), scales=w_scales[c][:, g, cols], in_=w_il[c, g][:, cols, :].rearrange("p n j -> p (n j)"))
+        def quantize_w(c, g, half=None):
+            cols = columns(half)
+            nc.vector.quantize_mx(
+                out=w_codes[c][:, g, cols].bitcast(E4M3X4),
+                scales=w_scales[c][:, g, cols],
+                in_=w_grouped[c, g][:, cols, :].rearrange("p n t -> p (n t)"),
+            )
+
 
         def product(kind, m, c):
             bank = psum.tile([P, WIDTH], F32, tag="bank", name="bank")
             banks[kind, m, c] = bank
-            s, o = (c, 0) if c < 2 else (2, WIDTH * (c - 2))
+            s, first = locate(c)
+            h, chunk_of_part = divmod(c, 2)
+            cols = slice(WIDTH * chunk_of_part, WIDTH * (chunk_of_part + 1))
             for g in range(GROUPS):
-                if kind == "g":
-                    rhs, rs = w_codes[c][:, g, :].bitcast(E4M3X4), w_scales[c][:, g, :]
-                elif kind == "d":
-                    k = 4 + 4 * g
-                    rhs, rs = d_codes[s][:, g, 4 * o:4 * (o + WIDTH)].bitcast(E4M3X4), d_planes[c // 2][k:P, WIDTH * (c % 2):WIDTH * (c % 2 + 1)]
+                if kind == "gate":
+                    rhs, rhs_scale = w_codes[c][:, g, :].bitcast(E4M3X4), w_scales[c][:, g, :]
+                elif kind == "domain":
+                    rhs = d_codes[s][:, g, 4 * first : 4 * (first + WIDTH)].bitcast(E4M3X4)
+                    rhs_scale = d_scales[h][ROWS * (g + 1) : P, cols]
                 else:
-                    rhs, rs = b_codes[s][:, g, 2 * o:2 * (o + WIDTH)].bitcast(E2M1X4), b_planes[c // 2][:, g, WIDTH * (c % 2):WIDTH * (c % 2 + 1)]
-                nc.tensor.matmul_mx(out=bank[:], lhsT=a_codes[m][:, g * P:(g + 1) * P].bitcast(E4M3X4), lhsT_scale=a_scales[m][:, g * P:(g + 1) * P], rhs=rhs, rhs_scale=rs, start=(g == 0), stop=(g == GROUPS - 1))
+                    rhs = b_codes[s][:, g, 2 * first : 2 * (first + WIDTH)].bitcast(E2M1X4)
+                    rhs_scale = b_scales[h][:, g, cols]
+                nc.tensor.matmul_mx(
+                    out=bank[:],
+                    lhsT=a_codes[m][:, g * P : (g + 1) * P].bitcast(E4M3X4),
+                    lhsT_scale=a_scales[m][:, g * P : (g + 1) * P],
+                    rhs=rhs,
+                    rhs_scale=rhs_scale,
+                    start=(g == 0),
+                    stop=(g == GROUPS - 1),
+                )
 
-        def squash(m, c):
-            t = keep.tile([P, WIDTH], F32, name=f"acc{m}{c}")
-            done[m, c] = t
-            nc.scalar.activation(out=t[:], in_=banks["g", m, c][:], func=ACT.Tanh, scale=0.5)
+        def half_tanh(m, c):
+            result[m, c] = keep.tile([P, WIDTH], F32, name=f"y{m}{c}")
+            nc.scalar.activation(out=result[m, c][:], in_=banks["gate", m, c][:], func=ACT.Tanh, scale=0.5)
 
-        def gated(m, c, h=None):
-            cols = slice(0, WIDTH) if h is None else slice(PIECE * h, PIECE * (h + 1))
-            t = done[m, c][:, cols]
-            nc.vector.scalar_tensor_tensor(out=t, in0=t, scalar=1.0, in1=banks["d", m, c][:, cols], op0=ALU.add, op1=ALU.mult)
+        def gated(m, c, half=None):
+            y = result[m, c][:, columns(half)]
+            nc.vector.scalar_tensor_tensor(
+                out=y, in0=y, scalar=1.0, in1=banks["domain", m, c][:, columns(half)], op0=ALU.add, op1=ALU.mult
+            )
 
-        def summed(m, c, h=None):
-            cols = slice(0, WIDTH) if h is None else slice(PIECE * h, PIECE * (h + 1))
-            t = done[m, c][:, cols]
-            nc.vector.scalar_tensor_tensor(out=t, in0=t, scalar=0.5, in1=banks["b", m, c][:, cols], op0=ALU.mult, op1=ALU.add)
+        def add_base(m, c, half=None):
+            y = result[m, c][:, columns(half)]
+            nc.vector.scalar_tensor_tensor(
+                out=y, in0=y, scalar=0.5, in1=banks["base", m, c][:, columns(half)], op0=ALU.mult, op1=ALU.add
+            )
 
-        def early(m, c):
-            t = done[m, c]
-            s, o = (c, 0) if c < 2 else (2, WIDTH * (c - 2))
-            nc.vector.scalar_tensor_tensor(out=t[:], in0=t[:], scalar=0.5, in1=r_raw[s][:, m, o:o + WIDTH], op0=ALU.mult, op1=ALU.add)
+        def add_resid_and_store(m, c, engine, half=None):
+            cols = columns(half)
+            y = result[m, c][:, cols]
+            s, first = locate(c)
+            engine.tensor_tensor(out=y, in0=y, in1=r_rows[s][:, m, first : first + WIDTH][:, cols], op=ALU.add)
+            nc.sync.dma_start(out=out[m * P : (m + 1) * P, c * WIDTH : (c + 1) * WIDTH][:, cols], in_=y)
 
-        def closing(m, c):
-            t = done[m, c]
-            nc.vector.tensor_tensor(out=t[:], in0=t[:], in1=banks["b", m, c][:], op=ALU.add)
 
-        def finish(m, c, eng, h=None):
-            cols = slice(0, WIDTH) if h is None else slice(PIECE * h, PIECE * (h + 1))
-            y = done[m, c][:, cols]
-            e = nc.gpsimd if eng == "G" else nc.vector
-            s, o = (c, 0) if c < 2 else (2, WIDTH * (c - 2))
-            e.tensor_tensor(out=y, in0=y, in1=r_raw[s][:, m, o:o + WIDTH][:, cols], op=ALU.add)
+        nc.vector.memset(d_scales[0][:].bitcast(I32), 0)
+        nc.vector.memset(dummy[:], 0.0)
+        nc.vector.memset(b_scales[0][:].rearrange("p g n -> p (g n)").bitcast(I32), 0)
+        nc.vector.memset(d_scales[1][:].bitcast(I32), 0)
+        nc.vector.memset(b_scales[1][:].rearrange("p g n -> p (g n)").bitcast(I32), 0)
+        make_identity(nc, ident[:])
 
-        def store(m, c, h=None):
-            cols = slice(0, WIDTH) if h is None else slice(PIECE * h, PIECE * (h + 1))
-            nc.sync.dma_start(out=out[m * P:(m + 1) * P, c * WIDTH:(c + 1) * WIDTH][:, cols], in_=done[m, c][:, cols])
+        load_z(0)
+        load_z(1)
+        load_scale()
+        load_w(0, 0)
+        load_w(0, 1)
+        load_z(2)
+        load_z(3)
+        load_d_scales(0)
+        load_d(0)
+        load_w(1, 0)
+        load_w(1, 1)
+        load_b_scales(0)
+        load_b(0)
+        load_d(1)
+        load_w(2, 0)
+        load_d_scales(1)
+        load_last_z()
+        load_w(2, 1)
+        load_b(1)
+        load_b_scales(1)
+        load_r(0)
+        load_r(1)
+        load_d(2)
+        load_b(2)
+        load_r(2)
 
-        ops = dict(early=early, closing=closing, init=init, load_s=load_s, warmup=warmup, load_scales=load_scales, load_z=load_z, load_w=load_w, load_b=load_b, load_d=load_d, load_r=load_r, gelu=gelu, turn=turn, weigh=weigh, quant_a=quant_a, lay=lay, quant_w=quant_w, product=product, squash=squash, gated=gated, summed=summed, finish=finish, store=store)
-        for step in PLAN:
-            ops[step[0]](*step[1:])
+        nc.scalar.activation(out=dummy[:], in_=dummy[:], func=ACT.Gelu_apprx_tanh)
+
+        turn(0)
+        turn(1)
+        gelu(0)
+        gelu(1)
+        multiply_scale(0, by_group=True)
+        interleave_w(0, 0, 0, "vector")
+        interleave_w(0, 1, 1, "vector")
+        interleave_w(0, 0, 1, "scalar")
+        interleave_w(0, 1, 0, "scalar")
+        quantize_a(0)
+        quantize_w(0, 1, 1)
+        multiply_scale(1)
+        quantize_w(0, 0, 0)
+        quantize_a(1)
+        turn(2)
+        turn(3)
+        product("domain", 0, 0)
+        product("domain", 1, 0)
+        quantize_w(0, 0, 1)
+        quantize_w(0, 1, 0)
+        gelu(2)
+        gelu(3)
+        multiply_scale(2)
+        multiply_scale(3)
+        interleave_w(1, 0, 0, "scalar")
+        product("gate", 0, 0)
+        product("gate", 1, 0)
+        product("base", 0, 0)
+        product("base", 1, 0)
+        quantize_a(2)
+        quantize_a(3)
+        interleave_w(1, 1, 0, "gpsimd")
+        half_tanh(0, 0)
+        half_tanh(1, 0)
+        gated(0, 0)
+        gated(1, 0)
+        interleave_w(1, 0, 1, "scalar")
+        interleave_w(1, 1, 1, "scalar")
+        add_base(0, 0)
+        quantize_w(1, 0)
+        add_base(1, 0)
+        quantize_w(1, 1)
+        for m in (0, 1):
+            add_resid_and_store(m, 0, nc.gpsimd)
+
+        steps = [(2, 0), (0, 1), (2, 1), (4, 0), (4, 1), (0, 2), (2, 2), (4, 2), (0, 3), (2, 3)]
+        prepare_a = (0, 1)
+        first_halves = {(2, 1): 2, (0, 2): 3}
+        second_halves = {(4, 0): 2, (2, 2): 3}
+        last_pair = (TILES - 2, TILES - 1)
+
+        for step in steps:
+            first_tile, c = step
+            pair = (first_tile, first_tile + 1)
+            if step == prepare_a:
+                for m in last_pair:
+                    turn(m)
+            for kind in ("gate", "domain", "base"):
+                for m in pair:
+                    product(kind, m, c)
+            if step == prepare_a:
+                for m in last_pair:
+                    gelu(m)
+            for todo, half in ((first_halves, 0), (second_halves, 1)):
+                if step in todo:
+                    for g in range(GROUPS):
+                        interleave_w(todo[step], g, half, "scalar")
+            for m in pair:
+                half_tanh(m, c)
+            if step == prepare_a:
+                for m in last_pair:
+                    multiply_scale(m)
+                for m in last_pair:
+                    quantize_a(m)
+            for m in pair:
+                gated(m, c)
+            if step in second_halves:
+                for g in range(GROUPS):
+                    quantize_w(second_halves[step], g)
+            for m in pair:
+                add_base(m, c)
+                add_resid_and_store(m, c, nc.gpsimd)
+
+        c = CHUNKS - 1
+        before_last, last = last_pair
+        for m in last_pair:
+            for kind in ("gate", "domain", "base"):
+                product(kind, m, c)
+        half_tanh(before_last, c)
+        gated(before_last, c)
+        half_tanh(last, c)
+        add_base(before_last, c)
+        add_resid_and_store(before_last, c, nc.gpsimd)
+        for half in HALVES:
+            gated(last, c, half)
+        for half in HALVES:
+            add_base(last, c, half)
+        for half in HALVES:
+            add_resid_and_store(last, c, nc.vector, half)

from contextlib import ExitStack

import concourse.mybir as mybir
from concourse.masks import make_identity

M, K, N = 768, 1024, 2048
FLOPS = 3 * 2 * M * K * N

F32 = mybir.dt.float32
BF16 = mybir.dt.bfloat16
U32 = mybir.dt.uint32
I32 = mybir.dt.int32
U8 = mybir.dt.uint8
E4M3X4 = mybir.dt.float8_e4m3fn_x4
E2M1X4 = mybir.dt.float4_e2m1fn_x4
ACT = mybir.ActivationFunctionType
ALU = mybir.AluOpType

P = 128
PACK = 4
GROUPS = 2
GROUP_K = P * PACK
TILES = M // P
WIDTH = 512
CHUNKS = N // WIDTH
HALF = WIDTH // 2
HALVES = (0, 1)
PART = N // 2
PARTS = range(N // PART)
QUADRANTS = 4
QUADRANT = P // QUADRANTS
ROWS = 4

SPANS = [(0, WIDTH), (WIDTH, 2 * WIDTH), (2 * WIDTH, N)]


def locate(c):
    s = min(c, len(SPANS) - 1)
    return s, WIDTH * c - SPANS[s][0]


def columns(half):
    return slice(0, WIDTH) if half is None else slice(HALF * half, HALF * (half + 1))


def tile_gated_adapter_up_s10_kernel(
    tc, z, scale, base_words, base_scales, domain_words, domain_scales, w_gate, resid, out
):
    nc = tc.nc
    with ExitStack() as ctx:
        keep = ctx.enter_context(tc.tile_pool(name="keep", bufs=1))
        work = ctx.enter_context(tc.tile_pool(name="work", bufs=4))
        psum = ctx.enter_context(tc.psum_pool(name="psum", bufs=8))
        ctx.enter_context(tc.manual_schedule())

        ident = keep.tile([P, P], F32, name="ident")
        dummy = keep.tile([P, 1], F32, name="dummy")
        scale_k = keep.tile([P, GROUPS, PACK], BF16, name="scale_k")
        z_one = [keep.tile([P, 1, K], BF16, name=f"z{m}") for m in range(TILES - 2)]
        z_two = keep.tile([P, 2, K], BF16, name="z4")
        z_rows = [t[:, 0, :] for t in z_one] + [z_two[:, i, :] for i in range(2)]
        a_codes = [keep.tile([P, GROUPS * P], U32, name=f"ac{m}", align_bytes=64) for m in range(TILES)]
        a_scales = [keep.tile([P, GROUPS * P], U8, name=f"as{m}", align_bytes=64) for m in range(TILES)]
        w_raw = [
            [keep.tile([P, PACK, hi - lo], BF16, name=f"w{s}{g}") for g in range(GROUPS)]
            for s, (lo, hi) in enumerate(SPANS)
        ]
        w_codes = [keep.tile([P, GROUPS, WIDTH], U32, name=f"wc{c}", align_bytes=64) for c in range(CHUNKS)]
        w_scales = [keep.tile([P, GROUPS, WIDTH], U8, name=f"ws{c}", align_bytes=64) for c in range(CHUNKS)]
        b_codes = [
            keep.tile([P, GROUPS, 2 * (hi - lo)], U8, name=f"bc{s}", align_bytes=64) for s, (lo, hi) in enumerate(SPANS)
        ]
        d_codes = [
            keep.tile([P, GROUPS, 4 * (hi - lo)], U8, name=f"dc{s}", align_bytes=64) for s, (lo, hi) in enumerate(SPANS)
        ]
        b_scales = [keep.tile([P, GROUPS, PART], U8, name=f"bs{h}", align_bytes=64) for h in PARTS]
        d_scales = [keep.tile([P, PART], U8, name=f"ds{h}", align_bytes=64) for h in PARTS]
        r_rows = [keep.tile([P, TILES, hi - lo], BF16, name=f"r{s}") for s, (lo, hi) in enumerate(SPANS)]

        turned, gelu_z, a_bf, w_grouped, banks, result = {}, {}, {}, {}, {}, {}


        def load_z(m):
            nc.sync.dma_start(out=z_one[m][:], in_=z[m * P : (m + 1) * P, :].rearrange("(n p) k -> p n k", p=P))

        def load_last_z():
            nc.sync.dma_start(out=z_two[:], in_=z[(TILES - 2) * P :, :].rearrange("(n p) k -> p n k", p=P))

        def load_scale():
            nc.sync.dma_start(out=scale_k[:], in_=scale.rearrange("(g p t) -> p g t", p=P, t=PACK))

        def load_w(s, g):
            lo, hi = SPANS[s]
            rows = w_gate[GROUP_K * g : GROUP_K * (g + 1), lo:hi]
            nc.sync.dma_start(out=w_raw[s][g][:], in_=rows.rearrange("(p t) n -> p t n", t=PACK))

        def load_b(s):
            lo, hi = SPANS[s]
            nc.sync.dma_start(out=b_codes[s][:], in_=base_words[:, :, 2 * lo : 2 * hi].rearrange("g p n -> p g n"))

        def load_d(s):
            lo, hi = SPANS[s]
            nc.sync.dma_start(out=d_codes[s][:], in_=domain_words[:, :, lo:hi, :].rearrange("g p n t -> p g (n t)"))

        def load_r(s):
            lo, hi = SPANS[s]
            nc.sync.dma_start(out=r_rows[s][:], in_=resid[:, lo:hi].rearrange("(m p) n -> p m n", p=P))

        def load_b_scales(h):
            int32s = slice(h * PART // 4, (h + 1) * PART // 4)
            for quad in range(QUADRANTS):
                first = QUADRANT * quad
                nc.sync.dma_start(
                    out=b_scales[h][first : first + ROWS].bitcast(I32),
                    in_=base_scales.bitcast(I32)[:, ROWS * quad : ROWS * (quad + 1), int32s].rearrange("g r n -> r g n"),
                )

        def load_d_scales(h):
            int32s = slice(h * PART // 4, (h + 1) * PART // 4)
            for quad in range(QUADRANTS):
                first = QUADRANT * quad + ROWS
                nc.sync.dma_start(
                    out=d_scales[h][first : first + GROUPS * ROWS, :].bitcast(I32),
                    in_=domain_scales.bitcast(I32)[:, ROWS * quad : ROWS * (quad + 1), int32s],
                )


        def turn(m):
            turned[m] = psum.tile([P, GROUPS, 2, P], F32, tag="bank", name="bank")
            pairs = z_rows[m].bitcast(F32)
            count = GROUP_K // 2
            for g in range(GROUPS):
                for u in range(2):
                    nc.tensor.transpose(turned[m][:, g, u, :], pairs[:, count * g + u : count * (g + 1) : 2], ident[:])

        def gelu(m):
            gelu_z[m] = work.tile([P, GROUPS, P, PACK], F32, tag="gelu", name="gelu", bufs=TILES)
            pairs = turned[m][:].rearrange("p g u r -> p (g u r)").bitcast(BF16)
            for g in range(GROUPS):
                nc.scalar.activation(
                    out=gelu_z[m][:, g].rearrange("p r (u e) -> p r u e", u=2),
                    in_=pairs[:, GROUP_K * g : GROUP_K * (g + 1)].rearrange("p (u r e) -> p r u e", u=2, e=2),
                    func=ACT.Gelu_apprx_tanh,
                )

        def multiply_scale(m, by_group=False):
            a_bf[m] = work.tile([P, GROUPS, P, PACK], BF16, tag="a_bf", name="a_bf", bufs=TILES, align_bytes=64)
            if by_group:
                for g in range(GROUPS):
                    factor = scale_k[:, g, :].unsqueeze(1).to_broadcast([P, P, PACK])
                    nc.vector.tensor_tensor(out=a_bf[m][:, g], in0=gelu_z[m][:, g], in1=factor, op=ALU.mult)
            else:
                factor = scale_k[:].unsqueeze(2).to_broadcast([P, GROUPS, P, PACK])
                nc.vector.tensor_tensor(out=a_bf[m][:], in0=gelu_z[m][:], in1=factor, op=ALU.mult)

        def quantize_a(m):
            nc.vector.quantize_mx(
                out=a_codes[m][:].bitcast(E4M3X4),
                scales=a_scales[m][:],
                in_=a_bf[m][:].rearrange("p g r t -> p (g r t)"),
            )

        def interleave_w(c, g, half, engine):
            if (c, g) not in w_grouped:
                w_grouped[c, g] = work.tile(
                    [P, WIDTH, PACK], BF16, tag="w_grouped", name="w_grouped", bufs=2 * GROUPS, align_bytes=64
                )
            s, first = locate(c)
            cols = slice(first + HALF * half, first + HALF * (half + 1))
            src = w_raw[s][g][:, :, cols].rearrange("p t (q i) -> p q t i", i=4)
            dst = w_grouped[c, g][:, columns(half), :].rearrange("p (q i) t -> p q t i", i=4)
            if engine == "scalar":
                nc.scalar.copy(out=dst, in_=src)
            elif engine == "vector":
                nc.vector.tensor_copy(out=dst, in_=src)
            else:
                nc.gpsimd.tensor_scalar(out=dst, in0=src, scalar1=1.0, scalar2=0.0, op0=ALU.mult, op1=ALU.add)

        def quantize_w(c, g, half=None):
            cols = columns(half)
            nc.vector.quantize_mx(
                out=w_codes[c][:, g, cols].bitcast(E4M3X4),
                scales=w_scales[c][:, g, cols],
                in_=w_grouped[c, g][:, cols, :].rearrange("p n t -> p (n t)"),
            )


        def product(kind, m, c):
            bank = psum.tile([P, WIDTH], F32, tag="bank", name="bank")
            banks[kind, m, c] = bank
            s, first = locate(c)
            h, chunk_of_part = divmod(c, 2)
            cols = slice(WIDTH * chunk_of_part, WIDTH * (chunk_of_part + 1))
            for g in range(GROUPS):
                if kind == "gate":
                    rhs, rhs_scale = w_codes[c][:, g, :].bitcast(E4M3X4), w_scales[c][:, g, :]
                elif kind == "domain":
                    rhs = d_codes[s][:, g, 4 * first : 4 * (first + WIDTH)].bitcast(E4M3X4)
                    rhs_scale = d_scales[h][ROWS * (g + 1) : P, cols]
                else:
                    rhs = b_codes[s][:, g, 2 * first : 2 * (first + WIDTH)].bitcast(E2M1X4)
                    rhs_scale = b_scales[h][:, g, cols]
                nc.tensor.matmul_mx(
                    out=bank[:],
                    lhsT=a_codes[m][:, g * P : (g + 1) * P].bitcast(E4M3X4),
                    lhsT_scale=a_scales[m][:, g * P : (g + 1) * P],
                    rhs=rhs,
                    rhs_scale=rhs_scale,
                    start=(g == 0),
                    stop=(g == GROUPS - 1),
                )

        def half_tanh(m, c):
            result[m, c] = keep.tile([P, WIDTH], F32, name=f"y{m}{c}")
            nc.scalar.activation(out=result[m, c][:], in_=banks["gate", m, c][:], func=ACT.Tanh, scale=0.5)

        def gated(m, c, half=None):
            y = result[m, c][:, columns(half)]
            nc.vector.scalar_tensor_tensor(
                out=y, in0=y, scalar=1.0, in1=banks["domain", m, c][:, columns(half)], op0=ALU.add, op1=ALU.mult
            )

        def add_base(m, c, half=None):
            y = result[m, c][:, columns(half)]
            nc.vector.scalar_tensor_tensor(
                out=y, in0=y, scalar=0.5, in1=banks["base", m, c][:, columns(half)], op0=ALU.mult, op1=ALU.add
            )

        def add_resid_and_store(m, c, engine, half=None):
            cols = columns(half)
            y = result[m, c][:, cols]
            s, first = locate(c)
            engine.tensor_tensor(out=y, in0=y, in1=r_rows[s][:, m, first : first + WIDTH][:, cols], op=ALU.add)
            nc.sync.dma_start(out=out[m * P : (m + 1) * P, c * WIDTH : (c + 1) * WIDTH][:, cols], in_=y)


        nc.vector.memset(d_scales[0][:].bitcast(I32), 0)
        nc.vector.memset(dummy[:], 0.0)
        nc.vector.memset(b_scales[0][:].rearrange("p g n -> p (g n)").bitcast(I32), 0)
        nc.vector.memset(d_scales[1][:].bitcast(I32), 0)
        nc.vector.memset(b_scales[1][:].rearrange("p g n -> p (g n)").bitcast(I32), 0)
        make_identity(nc, ident[:])

        load_z(0)
        load_z(1)
        load_scale()
        load_w(0, 0)
        load_w(0, 1)
        load_z(2)
        load_z(3)
        load_d_scales(0)
        load_d(0)
        load_w(1, 0)
        load_w(1, 1)
        load_b_scales(0)
        load_b(0)
        load_d(1)
        load_w(2, 0)
        load_d_scales(1)
        load_last_z()
        load_w(2, 1)
        load_b(1)
        load_b_scales(1)
        load_r(0)
        load_r(1)
        load_d(2)
        load_b(2)
        load_r(2)

        nc.scalar.activation(out=dummy[:], in_=dummy[:], func=ACT.Gelu_apprx_tanh)

        turn(0)
        turn(1)
        gelu(0)
        gelu(1)
        multiply_scale(0, by_group=True)
        interleave_w(0, 0, 0, "vector")
        interleave_w(0, 1, 1, "vector")
        interleave_w(0, 0, 1, "scalar")
        interleave_w(0, 1, 0, "scalar")
        quantize_a(0)
        quantize_w(0, 1, 1)
        multiply_scale(1)
        quantize_w(0, 0, 0)
        quantize_a(1)
        turn(2)
        turn(3)
        product("domain", 0, 0)
        product("domain", 1, 0)
        quantize_w(0, 0, 1)
        quantize_w(0, 1, 0)
        gelu(2)
        gelu(3)
        multiply_scale(2)
        multiply_scale(3)
        interleave_w(1, 0, 0, "scalar")
        product("gate", 0, 0)
        product("gate", 1, 0)
        product("base", 0, 0)
        product("base", 1, 0)
        quantize_a(2)
        quantize_a(3)
        interleave_w(1, 1, 0, "gpsimd")
        half_tanh(0, 0)
        half_tanh(1, 0)
        gated(0, 0)
        gated(1, 0)
        interleave_w(1, 0, 1, "scalar")
        interleave_w(1, 1, 1, "scalar")
        add_base(0, 0)
        quantize_w(1, 0)
        add_base(1, 0)
        quantize_w(1, 1)
        for m in (0, 1):
            add_resid_and_store(m, 0, nc.gpsimd)

        steps = [(2, 0), (0, 1), (2, 1), (4, 0), (4, 1), (0, 2), (2, 2), (4, 2), (0, 3), (2, 3)]
        prepare_a = (0, 1)
        first_halves = {(2, 1): 2, (0, 2): 3}
        second_halves = {(4, 0): 2, (2, 2): 3}
        last_pair = (TILES - 2, TILES - 1)

        for step in steps:
            first_tile, c = step
            pair = (first_tile, first_tile + 1)
            if step == prepare_a:
                for m in last_pair:
                    turn(m)
            for kind in ("gate", "domain", "base"):
                for m in pair:
                    product(kind, m, c)
            if step == prepare_a:
                for m in last_pair:
                    gelu(m)
            for todo, half in ((first_halves, 0), (second_halves, 1)):
                if step in todo:
                    for g in range(GROUPS):
                        interleave_w(todo[step], g, half, "scalar")
            for m in pair:
                half_tanh(m, c)
            if step == prepare_a:
                for m in last_pair:
                    multiply_scale(m)
                for m in last_pair:
                    quantize_a(m)
            for m in pair:
                gated(m, c)
            if step in second_halves:
                for g in range(GROUPS):
                    quantize_w(second_halves[step], g)
            for m in pair:
                add_base(m, c)
                add_resid_and_store(m, c, nc.gpsimd)

        c = CHUNKS - 1
        before_last, last = last_pair
        for m in last_pair:
            for kind in ("gate", "domain", "base"):
                product(kind, m, c)
        half_tanh(before_last, c)
        gated(before_last, c)
        half_tanh(last, c)
        add_base(before_last, c)
        add_resid_and_store(before_last, c, nc.gpsimd)
        for half in HALVES:
            gated(last, c, half)
        for half in HALVES:
            add_base(last, c, half)
        for half in HALVES:
            add_resid_and_store(last, c, nc.vector, half)
